import numpy as np
import ml_dtypes


def mxq(x, axis, fmt="e4m3"):
    dtype, down = {"e4m3": (ml_dtypes.float8_e4m3fn, 7), "e5m2": (ml_dtypes.float8_e5m2, 14)}[fmt]
    v = np.moveaxis(np.asarray(x, np.float32).astype(ml_dtypes.bfloat16).astype(np.float64), axis, -1)
    blocks = v.reshape(v.shape[:-1] + (-1, 32))
    amax = np.abs(blocks).max(-1, keepdims=True)
    byte = np.maximum(np.where(amax > 0, np.frexp(amax)[1] - 1 + 127, 0) - down, 1)
    scale = np.exp2(byte - 127.0)
    codes = (blocks / scale).astype(np.float32).astype(dtype).astype(np.float64)
    return np.moveaxis((codes * scale).reshape(v.shape), -1, axis)


WIDE = False


def mx_kscale(k):
    if not WIDE:
        return np.ones(k)
    levels = np.array([10, -10, 5, -5, 0])
    if k % 512:
        return np.exp2(np.random.permutation(np.resize(levels, k // 32))).repeat(32)
    a = np.empty((k // 512, 16))
    for p in range(k // 512):
        a[p, :8] = np.random.permutation(np.resize(levels, 8))
        for g in range(8):
            far = levels[np.abs(levels - a[p, g]) >= 10]
            a[p, g + 8] = far[np.random.randint(len(far))]
    return np.exp2(a.ravel()).repeat(32)


def f64(x):
    return np.asarray(x).astype(np.float64)


def striped(idx):
    return np.tile(idx.reshape(-1, 16).T, (8, 1)).astype(np.uint16)


def unstriped(offs):
    return offs[:16].T.reshape(-1).astype(np.int64)


def striped8(idx):
    return np.concatenate([x.reshape(-1, 16).T for x in idx]).astype(np.uint16)


def runs(offs, k):
    lists = np.stack([offs[16 * r : 16 * r + 16].T.reshape(-1) for r in range(8)]).astype(np.int64)
    return lists[np.arange(k) % 512 // 64]


def pack_weight(w):
    k, n = w.shape
    w = f64(np.asarray(w, np.float32).astype(ml_dtypes.bfloat16)).reshape(k // 32, 32, n)
    amax = np.abs(w).max(1)
    byte = np.clip(np.where(amax > 0, np.frexp(amax)[1] - 1 + 127 - 7, 1), 1, 254)
    scaled = (w * np.exp2(127.0 - byte)[:, None, :]).reshape(k, n).astype(np.float32)
    words = np.ascontiguousarray(scaled.reshape(k // 512, 128, 4, n).transpose(0, 1, 3, 2)).astype(ml_dtypes.float8_e4m3fn).view(np.uint8)
    return words, np.ascontiguousarray(byte.astype(np.uint8).reshape(k // 512, 16, n))


def unpack_weight(words, scales):
    g, p, n, _ = words.shape
    vals = np.ascontiguousarray(words).view(ml_dtypes.float8_e4m3fn).astype(np.float64) * np.repeat(np.exp2(scales.astype(np.float64) - 127.0), 8, axis=1)[..., None]
    return vals.transpose(0, 1, 3, 2).reshape(g * 512, n)


E2M1 = np.array([0.0, 0.5, 1.0, 1.5, 2.0, 3.0, 4.0, 6.0, -0.0, -0.5, -1.0, -1.5, -2.0, -3.0, -4.0, -6.0])


def pack_fp4(w):
    k, n = w.shape
    w = f64(np.asarray(w, np.float32).astype(ml_dtypes.bfloat16)).reshape(k // 32, 32, n)
    amax = np.abs(w).max(1)
    mant, ex = np.frexp(amax / 6.0)
    byte = np.clip(np.where(amax > 0, np.where(mant > 0.5, ex, ex - 1) + 127, 1), 1, 254)
    scaled = (w * np.exp2(127.0 - byte)[:, None, :]).reshape(k, n).astype(np.float32)
    c = np.ascontiguousarray(scaled.reshape(k // 512, 128, 4, n).transpose(0, 1, 3, 2)).astype(ml_dtypes.float4_e2m1fn).view(np.uint8) & 0xF
    words = (c[..., 0::2] | (c[..., 1::2] << 4)).reshape(k // 512, 128, 2 * n)
    return np.ascontiguousarray(words), np.ascontiguousarray(byte.astype(np.uint8).reshape(k // 512, 16, n))


def unpack_fp4(words, scales):
    g, _, n = scales.shape
    words = np.ascontiguousarray(words).reshape(g, 128, n, 2)
    nib = np.empty((g, 128, n, 4), np.uint8)
    nib[..., 0::2] = words & 0xF
    nib[..., 1::2] = words >> 4
    vals = E2M1[nib] * np.repeat(np.exp2(scales.astype(np.float64) - 127.0), 8, axis=1)[..., None]
    return vals.transpose(0, 1, 3, 2).reshape(g * 512, n)


def relu(v):
    return np.maximum(v, 0.0)

def planes(y):
    n, m = y.shape
    v = y.astype(np.float32).astype(ml_dtypes.bfloat16).astype(np.float64).reshape(n // 32, 32, m)
    top = np.abs(v).max(1)
    byte = np.clip(np.where(top > 0, np.frexp(top)[1] - 1 + 127 - 7, 1), 1, 254)
    codes = (v * np.exp2(127.0 - byte)[:, None, :]).reshape(n, m).astype(np.float32).astype(ml_dtypes.float8_e4m3fn).view(np.uint8)
    words = codes.reshape(n // 512, 128, 4, m).transpose(0, 1, 3, 2)
    return np.ascontiguousarray(words), np.ascontiguousarray(byte.astype(np.uint8).reshape(n // 512, 16, m))


K, T, S, V, N, G, H = 512, 2048, 1024, 512, 512, 2048, 512


def setup_inputs():
    n = np.random.standard_normal
    s = mx_kscale(K)[:, None]
    u = mx_kscale(H)
    packed_xT = pack_weight(n((K, T)) * s)
    packed_dT = pack_weight(n((K, G)) / s)
    packed_w1 = pack_fp4(n((H, N)) / np.sqrt(H) / u[:, None])
    return {
        "x_words": packed_xT[0],
        "x_scales": packed_xT[1],
        "d_words": packed_dT[0],
        "d_scales": packed_dT[1],
        "gn": (np.random.uniform(0.5, 1.5, (H, 1)) * u[:, None]).astype(np.float32),
        "w1_words": packed_w1[0],
        "w1_scales": packed_w1[1],
        "offs": striped(np.random.permutation(T)[:S]),
        "kidx": striped8(np.random.randint(0, G, (8, H))),
    }


def reference(x_words, x_scales, d_words, d_scales, gn, w1_words, w1_scales, offs, kidx):
    d_kidx = unpack_weight(d_words, d_scales)[np.arange(K)[:, None], runs(kidx, K)]
    xq = unpack_weight(x_words, x_scales)[:, unstriped(offs)]
    s = 0.0625 * (d_kidx.T @ xq)
    mx = s.reshape(H, V, 2).max(axis=2)
    z = f64(gn) * relu(mx)
    out_0 = unpack_fp4(w1_words, w1_scales).T @ mxq(z, 0, "e4m3")
    return (out_0,) + planes(out_0)

@@ -1,0 +1,224 @@
+from contextlib import ExitStack
+
+import concourse.mybir as mybir
+
+K, T, S, V, N, G, H = 512, 2048, 1024, 512, 512, 2048, 512
+FLOPS = 2 * K * H * S + 2 * H * N * V
+
+F32 = mybir.dt.float32
+BF16 = mybir.dt.bfloat16
+I32 = mybir.dt.int32
+U32 = mybir.dt.uint32
+U16 = mybir.dt.uint16
+U8 = mybir.dt.uint8
+FP8X4 = mybir.dt.float8_e4m3fn_x4
+FP4X4 = mybir.dt.float4_e2m1fn_x4
+ALU = mybir.AluOpType
+ACT = mybir.ActivationFunctionType
+
+P = 128
+PACK = 4
+LIST = 16
+SCORE_SCALE = 0.0625
+CHUNK_V = 128
+CHUNK_J = 2 * CHUNK_V
+CHUNKS = V // CHUNK_V
+BANK_J = 128
+BANK_V = BANK_J // 2
+
+
+def tile_picked_scorepool_relu_po_kernel(
+    tc, x_words, x_scales, d_words, d_scales, gn, w1_words, w1_scales, offs, kidx, out_0, out_1, out_2
+):
+    nc = tc.nc
+    with ExitStack() as ctx:
+        keep = ctx.enter_context(tc.tile_pool(name="keep", bufs=1))
+        score_psum = ctx.enter_context(tc.psum_pool(name="score_psum", bufs=6))
+        out_psum = ctx.enter_context(tc.psum_pool(name="out_psum", bufs=2))
+
+        kidx_sb = keep.tile([P, H // LIST], U16, name="kidx_sb")
+        offs_sb = keep.tile([P, S // LIST], U16, name="offs_sb")
+        d_scale_table = keep.tile([P, G], U8, name="d_scale_table", align_bytes=64)
+        x_scale_table = keep.tile([P, T], U8, name="x_scale_table", align_bytes=64)
+        d_word_table = keep.tile([P, G], U32, name="d_word_table", align_bytes=64)
+        x_word_table = keep.tile([P, T], U32, name="x_word_table", align_bytes=64)
+        w_words_in = keep.tile([P, 2 * N], U8, name="w_words_in", align_bytes=64)
+        w_scales_in = keep.tile([P, N], U8, name="w_scales_in", align_bytes=64)
+        gains = keep.tile([P, PACK], F32, name="gains")
+        d_plane = keep.tile([P, H], U8, name="d_plane", align_bytes=64)
+
+        w_plane = keep.tile([P, N], U8, name="w_plane", align_bytes=64)
+        nc.vector.memset(d_plane[:].bitcast(I32), 0)
+        nc.vector.memset(w_plane[:].bitcast(I32), 0)
+
+        def by_block(scales):
+            rows = scales[0].bitcast(I32)
+            return rows.unsqueeze(1).to_broadcast([16, 8, rows.shape[1]])
+
+        def to_plane(plane, dealt, queues):
+            for r in range(4):
+                queues[r % len(queues)].dma_start(plane[r:P:32, :].bitcast(I32), dealt[8 * r : P : 32, :].bitcast(I32))
+
+        nc.sync.dma_start(kidx_sb[:], kidx)
+        nc.sync.dma_start(d_scale_table[:].bitcast(I32), by_block(d_scales))
+        nc.sync.dma_start(offs_sb[:], offs)
+        for q in range(4):
+            rows = x_scales[0, 4 * q : 4 * q + 4, :].bitcast(I32)
+            nc.sync.dma_start(
+                x_scale_table[32 * q : 32 * q + 32, :].bitcast(I32), rows.unsqueeze(0).to_broadcast([8, 4, T // 4])
+            )
+        nc.sync.dma_start(d_word_table[:].bitcast(I32), d_words[0].rearrange("p c r -> p (c r)").bitcast(I32))
+        nc.sync.dma_start(x_word_table[:].bitcast(I32), x_words[0].rearrange("p c r -> p (c r)").bitcast(I32))
+        nc.sync.dma_start(w_scales_in[:].bitcast(I32), by_block(w1_scales))
+        nc.sync.dma_start(w_words_in[:].bitcast(I32), w1_words[0].bitcast(I32))
+        nc.sync.dma_start(gains[:], gn.rearrange("(p t) o -> p (t o)", t=PACK))
+
+        d_scales_picked = keep.tile([P, H], U8, name="d_scales_picked", align_bytes=64)
+        d_scales_dealt = keep.tile([P, H], U8, name="d_scales_dealt", align_bytes=64)
+        d_picked = keep.tile([P, H], U32, name="d_picked", align_bytes=64)
+        d_codes = keep.tile([P, H], U32, name="d_codes", align_bytes=64)
+        w_codes = keep.tile([P, 2 * N], U8, name="w_codes", align_bytes=64)
+        w_scales_dealt = keep.tile([P, N], U8, name="w_scales_dealt", align_bytes=64)
+        x_planes = [keep.tile([P, CHUNK_J], U8, name="x_plane%d" % c, align_bytes=64) for c in range(CHUNKS)]
+        x_codes = [keep.tile([P, CHUNK_J], U32, name="x_codes%d" % c, align_bytes=64) for c in range(CHUNKS)]
+        firsts = [keep.tile([P, CHUNK_V, PACK], F32, name="first%d" % c) for c in range(CHUNKS)]
+        pooled = [keep.tile([P, CHUNK_V, PACK], F32, name="pooled%d" % c) for c in range(CHUNKS)]
+        z_bf = [keep.tile([P, CHUNK_V, PACK], BF16, name="z_bf%d" % c, align_bytes=64) for c in range(CHUNKS)]
+        z_codes = [keep.tile([P, CHUNK_V], U32, name="z_codes%d" % c, align_bytes=64) for c in range(CHUNKS)]
+        z_planes = [keep.tile([P, CHUNK_V], U8, name="z_plane%d" % c, align_bytes=64) for c in range(CHUNKS)]
+        y_f32 = [keep.tile([P, PACK, CHUNK_V], F32, name="y_f32_%d" % c) for c in range(CHUNKS)]
+        y_bf = [keep.tile([P, CHUNK_V, PACK], BF16, name="y_bf%d" % c, align_bytes=64) for c in range(CHUNKS)]
+        y_codes = keep.tile([P, V], U32, name="y_codes", align_bytes=64)
+        y_plane = keep.tile([P, V], U8, name="y_plane", align_bytes=64)
+
+        def token_list(c):
+            return offs_sb[:, c * CHUNK_J // LIST : (c + 1) * CHUNK_J // LIST]
+
+        def gather_x_scales(c):
+            nc.vector.tensor_copy(x_planes[c][:], x_scale_table[:].indirect(token_list(c)))
+
+        def scores(c):
+            nc.vector.tensor_copy(x_codes[c][:], x_word_table[:].indirect(token_list(c)))
+            banks = []
+            for b in range(CHUNK_J // BANK_J):
+                bank = score_psum.tile([P, PACK, BANK_J], F32, name="score_bank")
+                cols = slice(b * BANK_J, (b + 1) * BANK_J)
+                for t in range(PACK):
+                    keys = slice(t * P, (t + 1) * P)
+                    nc.tensor.matmul_mx(
+                        out=bank[:, t, :],
+                        lhsT=d_codes[:, keys].bitcast(FP8X4),
+                        lhsT_scale=d_plane[:, keys],
+                        rhs=x_codes[c][:, cols].bitcast(FP8X4),
+                        rhs_scale=x_planes[c][:, cols],
+                        start=True,
+                        stop=True,
+                    )
+                nc.scalar.activation(
+                    firsts[c][:, b * BANK_V : (b + 1) * BANK_V, :],
+                    bank[:, :, 0:BANK_J:2].rearrange("p t v -> p v t"),
+                    ACT.Relu,
+                )
+                banks.append(bank)
+            return banks
+
+        def pool(c, banks):
+            for b, bank in enumerate(banks):
+                rows = slice(b * BANK_V, (b + 1) * BANK_V)
+                nc.vector.tensor_tensor(
+                    pooled[c][:, rows, :],
+                    bank[:, :, 1:BANK_J:2].rearrange("p t v -> p v t"),
+                    firsts[c][:, rows, :],
+                    ALU.max,
+                )
+
+        def weigh(c):
+            nc.vector.scalar_tensor_tensor(
+                z_bf[c][:],
+                pooled[c][:],
+                SCORE_SCALE,
+                gains[:].unsqueeze(1).to_broadcast([P, CHUNK_V, PACK]),
+                ALU.mult,
+                ALU.mult,
+            )
+
+        def values(c):
+            nc.vector.quantize_mx(
+                out=z_codes[c][:].bitcast(FP8X4), scales=z_planes[c][:], in_=z_bf[c][:].rearrange("p v t -> p (v t)")
+            )
+            bank = out_psum.tile([P, PACK, CHUNK_V], F32, name="out_bank")
+            for t in range(PACK):
+                nc.tensor.matmul_mx(
+                    out=bank[:, t, :],
+                    lhsT=w_codes[:, 2 * t * P : 2 * (t + 1) * P].bitcast(FP4X4),
+                    lhsT_scale=w_plane[:, t * P : (t + 1) * P],
+                    rhs=z_codes[c][:].bitcast(FP8X4),
+                    rhs_scale=z_planes[c][:],
+                    start=True,
+                    stop=True,
+                )
+            cols = slice(c * CHUNK_V, (c + 1) * CHUNK_V)
+            if c < CHUNKS - 1:
+                nc.scalar.copy(y_bf[c][:], bank[:].rearrange("p t v -> p v t"))
+            nc.scalar.copy(y_f32[c][:], bank[:])
+            nc.sync.dma_start(out_0.rearrange("(p t) v -> p t v", t=PACK)[:, :, cols], y_f32[c][:])
+            if c == CHUNKS - 1:
+                nc.vector.tensor_copy(
+                    y_bf[c][:].rearrange("p (u i) t -> p u t i", i=4), y_f32[c][:].rearrange("p t (u i) -> p u t i", i=4)
+                )
+
+        def quantise_out(c):
+            cols = slice(c * CHUNK_V, (c + 1) * CHUNK_V)
+            nc.vector.quantize_mx(
+                out=y_codes[:, cols].bitcast(FP8X4), scales=y_plane[:, cols], in_=y_bf[c][:].rearrange("p v t -> p (v t)")
+            )
+
+        nc.vector.tensor_copy(d_scales_picked[:], d_scale_table[:].indirect(kidx_sb[:]))
+        gather_x_scales(0)
+        nc.vector.tensor_copy(
+            d_scales_dealt[:].rearrange("p (t m) -> p t m", t=PACK),
+            d_scales_picked[:].rearrange("p (m t) -> p t m", t=PACK),
+        )
+        to_plane(d_plane, d_scales_dealt, [nc.scalar])
+        gather_x_scales(1)
+        nc.vector.tensor_copy(d_picked[:], d_word_table[:].indirect(kidx_sb[:]))
+        gather_x_scales(2)
+        nc.vector.tensor_copy(
+            d_codes[:].rearrange("p (t m) -> p m t", t=PACK), d_picked[:].rearrange("p (m t) -> p m t", t=PACK)
+        )
+        banks0 = scores(0)
+        nc.vector.tensor_copy(
+            w_scales_dealt[:].rearrange("p (t m) -> p t m", t=PACK), w_scales_in[:].rearrange("p (m t) -> p t m", t=PACK)
+        )
+        to_plane(w_plane, w_scales_dealt, [nc.sync])
+        banks1 = scores(1)
+        gather_x_scales(3)
+        pool(0, banks0)
+        nc.vector.tensor_copy(
+            w_codes[:].rearrange("p (t m b) -> p t m b", t=PACK, b=2),
+            w_words_in[:].rearrange("p (m t b) -> p t m b", t=PACK, b=2),
+        )
+        weigh(0)
+        banks2 = scores(2)
+        values(0)
+        pool(1, banks1)
+        banks3 = scores(3)
+        weigh(1)
+        pool(2, banks2)
+        values(1)
+        weigh(2)
+        quantise_out(0)
+        values(2)
+        pool(3, banks3)
+        quantise_out(1)
+        weigh(3)
+        words_out = out_1[0].rearrange("p c r -> p (c r)").bitcast(I32)
+        quantise_out(2)
+        values(3)
+        early = (CHUNKS - 1) * CHUNK_V
+        nc.sync.dma_start(words_out[:, 0:early], y_codes[:, 0:early].bitcast(I32))
+        quantise_out(3)
+        nc.sync.dma_start(words_out[:, early:V], y_codes[:, early:V].bitcast(I32))
+        for q in range(4):
+            queue = nc.scalar if q % 2 == 0 else nc.sync
+            queue.dma_start(out_2[0, 4 * q : 4 * q + 4, :].bitcast(I32), y_plane[32 * q : 32 * q + 4, :].bitcast(I32))

@@ -33,23 +33,23 @@ def tile_picked_scorepool_relu_po_kernel(
     nc = tc.nc
     with ExitStack() as ctx:
         keep = ctx.enter_context(tc.tile_pool(name="keep", bufs=1))
-        score_psum = ctx.enter_context(tc.psum_pool(name="score_psum", bufs=6))
-        out_psum = ctx.enter_context(tc.psum_pool(name="out_psum", bufs=2))
+        reused = ctx.enter_context(tc.tile_pool(name="reused", bufs=1))
+        score_psum = ctx.enter_context(tc.psum_pool(name="score_psum", bufs=5))
+        out_psum = ctx.enter_context(tc.psum_pool(name="out_psum", bufs=3))
 
         kidx_sb = keep.tile([P, H // LIST], U16, name="kidx_sb")
         offs_sb = keep.tile([P, S // LIST], U16, name="offs_sb")
         d_scale_table = keep.tile([P, G], U8, name="d_scale_table", align_bytes=64)
         x_scale_table = keep.tile([P, T], U8, name="x_scale_table", align_bytes=64)
-        d_word_table = keep.tile([P, G], U32, name="d_word_table", align_bytes=64)
-        x_word_table = keep.tile([P, T], U32, name="x_word_table", align_bytes=64)
-        w_words_in = keep.tile([P, 2 * N], U8, name="w_words_in", align_bytes=64)
-        w_scales_in = keep.tile([P, N], U8, name="w_scales_in", align_bytes=64)
-        gains = keep.tile([P, PACK], F32, name="gains")
+        d_word_table = reused.tile([P, G], U32, name="d_word_table", offset=0, align_bytes=64)
+        x_word_table = reused.tile([P, T], U32, name="x_word_table", offset=4 * G, align_bytes=64)
+        w_words_in = keep.tile([P, 2 * N], U8, name="w_words_in", tag="w_words_then_gains", align_bytes=64)
+        w_scales_in = reused.tile([P, N], U8, name="w_scales_in", offset=4 * G, align_bytes=64)
         d_plane = keep.tile([P, H], U8, name="d_plane", align_bytes=64)
 
-        w_plane = keep.tile([P, N], U8, name="w_plane", align_bytes=64)
+        nc.vector.memset(d_scale_table[:].bitcast(I32), 0)
+        nc.vector.memset(x_scale_table[:].bitcast(I32), 0)
         nc.vector.memset(d_plane[:].bitcast(I32), 0)
-        nc.vector.memset(w_plane[:].bitcast(I32), 0)
 
         def by_block(scales):
             rows = scales[0].bitcast(I32)
@@ -59,27 +59,24 @@ def tile_picked_scorepool_relu_po_kernel(
             for r in range(4):
                 queues[r % len(queues)].dma_start(plane[r:P:32, :].bitcast(I32), dealt[8 * r : P : 32, :].bitcast(I32))
 
-        nc.sync.dma_start(kidx_sb[:], kidx)
-        nc.sync.dma_start(d_scale_table[:].bitcast(I32), by_block(d_scales))
-        nc.sync.dma_start(offs_sb[:], offs)
-        for q in range(4):
-            rows = x_scales[0, 4 * q : 4 * q + 4, :].bitcast(I32)
-            nc.sync.dma_start(
-                x_scale_table[32 * q : 32 * q + 32, :].bitcast(I32), rows.unsqueeze(0).to_broadcast([8, 4, T // 4])
-            )
-        nc.sync.dma_start(d_word_table[:].bitcast(I32), d_words[0].rearrange("p c r -> p (c r)").bitcast(I32))
-        nc.sync.dma_start(x_word_table[:].bitcast(I32), x_words[0].rearrange("p c r -> p (c r)").bitcast(I32))
         nc.sync.dma_start(w_scales_in[:].bitcast(I32), by_block(w1_scales))
-        nc.sync.dma_start(w_words_in[:].bitcast(I32), w1_words[0].bitcast(I32))
-        nc.sync.dma_start(gains[:], gn.rearrange("(p t) o -> p (t o)", t=PACK))
+        for half in (slice(0, N), slice(N, 2 * N)):
+            nc.sync.dma_start(w_words_in[:, half].bitcast(I32), w1_words[0, :, half].bitcast(I32))
+        nc.sync.dma_start(kidx_sb[:], kidx)
+        nc.sync.dma_start(offs_sb[:], offs)
+        nc.sync.dma_start(d_scale_table[0:P:8, :].bitcast(I32), d_scales[0].bitcast(I32))
+        nc.sync.dma_start(d_word_table[:].bitcast(I32), d_words[0].rearrange("p c r -> p (c r)").bitcast(I32))
+        for q in range(4):
+            nc.sync.dma_start(
+                x_scale_table[32 * q : 32 * q + 4, :].bitcast(I32), x_scales[0, 4 * q : 4 * q + 4, :].bitcast(I32)
+            )
 
-        d_scales_picked = keep.tile([P, H], U8, name="d_scales_picked", align_bytes=64)
+        d_scales_picked = keep.tile([P, H], U8, name="d_scales_picked", tag="scale_bytes", align_bytes=64)
         d_scales_dealt = keep.tile([P, H], U8, name="d_scales_dealt", align_bytes=64)
         d_picked = keep.tile([P, H], U32, name="d_picked", align_bytes=64)
         d_codes = keep.tile([P, H], U32, name="d_codes", align_bytes=64)
         w_codes = keep.tile([P, 2 * N], U8, name="w_codes", align_bytes=64)
         w_scales_dealt = keep.tile([P, N], U8, name="w_scales_dealt", align_bytes=64)
-        x_planes = [keep.tile([P, CHUNK_J], U8, name="x_plane%d" % c, align_bytes=64) for c in range(CHUNKS)]
         x_codes = [keep.tile([P, CHUNK_J], U32, name="x_codes%d" % c, align_bytes=64) for c in range(CHUNKS)]
         firsts = [keep.tile([P, CHUNK_V, PACK], F32, name="first%d" % c) for c in range(CHUNKS)]
         pooled = [keep.tile([P, CHUNK_V, PACK], F32, name="pooled%d" % c) for c in range(CHUNKS)]
@@ -146,26 +143,42 @@ def tile_picked_scorepool_relu_po_kernel(
             nc.vector.quantize_mx(
                 out=z_codes[c][:].bitcast(FP8X4), scales=z_planes[c][:], in_=z_bf[c][:].rearrange("p v t -> p (v t)")
             )
-            bank = out_psum.tile([P, PACK, CHUNK_V], F32, name="out_bank")
-            for t in range(PACK):
-                nc.tensor.matmul_mx(
-                    out=bank[:, t, :],
-                    lhsT=w_codes[:, 2 * t * P : 2 * (t + 1) * P].bitcast(FP4X4),
-                    lhsT_scale=w_plane[:, t * P : (t + 1) * P],
-                    rhs=z_codes[c][:].bitcast(FP8X4),
-                    rhs_scale=z_planes[c][:],
-                    start=True,
-                    stop=True,
-                )
             cols = slice(c * CHUNK_V, (c + 1) * CHUNK_V)
+            out_rows = out_0.rearrange("(p t) v -> p t v", t=PACK)
+
+            def product(bank, first, count):
+                for t in range(first, first + count):
+                    nc.tensor.matmul_mx(
+                        out=bank[:, t - first, :],
+                        lhsT=w_codes[:, 2 * t * P : 2 * (t + 1) * P].bitcast(FP4X4),
+                        lhsT_scale=w_plane[:, t * P : (t + 1) * P],
+                        rhs=z_codes[c][:].bitcast(FP8X4),
+                        rhs_scale=z_planes[c][:],
+                        start=True,
+                        stop=True,
+                    )
+
             if c < CHUNKS - 1:
-                nc.scalar.copy(y_bf[c][:], bank[:].rearrange("p t v -> p v t"))
-            nc.scalar.copy(y_f32[c][:], bank[:])
-            nc.sync.dma_start(out_0.rearrange("(p t) v -> p t v", t=PACK)[:, :, cols], y_f32[c][:])
-            if c == CHUNKS - 1:
-                nc.vector.tensor_copy(
-                    y_bf[c][:].rearrange("p (u i) t -> p u t i", i=4), y_f32[c][:].rearrange("p t (u i) -> p u t i", i=4)
-                )
+                bank = out_psum.tile([P, PACK, CHUNK_V], F32, name="out_bank")
+                product(bank, 0, PACK)
+                if c < CHUNKS - 2:
+                    nc.scalar.copy(y_bf[c][:], bank[:].rearrange("p t v -> p v t"))
+                nc.scalar.copy(y_f32[c][:], bank[:])
+                nc.sync.dma_start(out_rows[:, :, cols], y_f32[c][:])
+            else:
+                low = out_psum.tile([P, 2, CHUNK_V], F32, name="out_bank")
+                product(low, 0, 2)
+                nc.scalar.copy(y_f32[c][:, 0:2, :], low[:])
+                nc.scalar.dma_start(out_rows[:, 0:2, cols], y_f32[c][:, 0:2, :])
+                high = out_psum.tile([P, 2, CHUNK_V], F32, name="out_bank")
+                product(high, 2, 2)
+                nc.vector.tensor_copy(y_f32[c][:, 2:4, :], high[:])
+                nc.sync.dma_start(out_rows[:, 2:4, cols], y_f32[c][:, 2:4, :])
+
+        def round_out(c):
+            nc.vector.tensor_copy(
+                y_bf[c][:].rearrange("p (u i) t -> p u t i", i=4), y_f32[c][:].rearrange("p t (u i) -> p u t i", i=4)
+            )
 
         def quantise_out(c):
             cols = slice(c * CHUNK_V, (c + 1) * CHUNK_V)
@@ -173,50 +186,60 @@ def tile_picked_scorepool_relu_po_kernel(
                 out=y_codes[:, cols].bitcast(FP8X4), scales=y_plane[:, cols], in_=y_bf[c][:].rearrange("p v t -> p (v t)")
             )
 
+        nc.vector.tensor_copy(
+            w_scales_dealt[:].rearrange("p (t m) -> p t m", t=PACK), w_scales_in[:].rearrange("p (m t) -> p t m", t=PACK)
+        )
+        nc.sync.dma_start(x_word_table[:].bitcast(I32), x_words[0].rearrange("p c r -> p (c r)").bitcast(I32))
+        nc.vector.tensor_copy(
+            w_codes[:].rearrange("p (t m b) -> p t m b", t=PACK, b=2),
+            w_words_in[:].rearrange("p (m t b) -> p t m b", t=PACK, b=2),
+        )
+        gains = keep.tile([P, PACK], F32, name="gains", tag="w_words_then_gains", align_bytes=64)
+        nc.sync.dma_start(gains[:], gn.rearrange("(p t) o -> p (t o)", t=PACK))
         nc.vector.tensor_copy(d_scales_picked[:], d_scale_table[:].indirect(kidx_sb[:]))
-        gather_x_scales(0)
         nc.vector.tensor_copy(
             d_scales_dealt[:].rearrange("p (t m) -> p t m", t=PACK),
             d_scales_picked[:].rearrange("p (m t) -> p t m", t=PACK),
         )
         to_plane(d_plane, d_scales_dealt, [nc.scalar])
-        gather_x_scales(1)
+        w_plane = keep.tile([P, N], U8, name="w_plane", tag="scale_bytes", align_bytes=64)
+        nc.gpsimd.memset(w_plane[:].bitcast(I32), 0)
+        to_plane(w_plane, w_scales_dealt, [nc.sync])
         nc.vector.tensor_copy(d_picked[:], d_word_table[:].indirect(kidx_sb[:]))
-        gather_x_scales(2)
+        x_planes = [
+            reused.tile([P, CHUNK_J], U8, name="x_plane%d" % c, offset=c * CHUNK_J, align_bytes=64) for c in range(CHUNKS)
+        ]
+        gather_x_scales(0)
         nc.vector.tensor_copy(
             d_codes[:].rearrange("p (t m) -> p m t", t=PACK), d_picked[:].rearrange("p (m t) -> p m t", t=PACK)
         )
         banks0 = scores(0)
-        nc.vector.tensor_copy(
-            w_scales_dealt[:].rearrange("p (t m) -> p t m", t=PACK), w_scales_in[:].rearrange("p (m t) -> p t m", t=PACK)
-        )
-        to_plane(w_plane, w_scales_dealt, [nc.sync])
+        gather_x_scales(1)
         banks1 = scores(1)
+        gather_x_scales(2)
+        banks2 = scores(2)
         gather_x_scales(3)
         pool(0, banks0)
-        nc.vector.tensor_copy(
-            w_codes[:].rearrange("p (t m b) -> p t m b", t=PACK, b=2),
-            w_words_in[:].rearrange("p (m t b) -> p t m b", t=PACK, b=2),
-        )
         weigh(0)
-        banks2 = scores(2)
+        banks3 = scores(3)
         values(0)
         pool(1, banks1)
-        banks3 = scores(3)
         weigh(1)
         pool(2, banks2)
         values(1)
         weigh(2)
-        quantise_out(0)
-        values(2)
         pool(3, banks3)
-        quantise_out(1)
+        values(2)
+        quantise_out(0)
         weigh(3)
+        quantise_out(1)
         words_out = out_1[0].rearrange("p c r -> p (c r)").bitcast(I32)
-        quantise_out(2)
-        values(3)
-        early = (CHUNKS - 1) * CHUNK_V
+        early = V // 2
         nc.sync.dma_start(words_out[:, 0:early], y_codes[:, 0:early].bitcast(I32))
+        values(3)
+        round_out(2)
+        quantise_out(2)
+        round_out(3)
         quantise_out(3)
         nc.sync.dma_start(words_out[:, early:V], y_codes[:, early:V].bitcast(I32))
         for q in range(4):

@@ -33,7 +33,6 @@ def tile_picked_scorepool_relu_po_kernel(
     nc = tc.nc
     with ExitStack() as ctx:
         keep = ctx.enter_context(tc.tile_pool(name="keep", bufs=1))
-        reused = ctx.enter_context(tc.tile_pool(name="reused", bufs=1))
         score_psum = ctx.enter_context(tc.psum_pool(name="score_psum", bufs=5))
         out_psum = ctx.enter_context(tc.psum_pool(name="out_psum", bufs=3))
 
@@ -41,10 +40,9 @@ def tile_picked_scorepool_relu_po_kernel(
         offs_sb = keep.tile([P, S // LIST], U16, name="offs_sb")
         d_scale_table = keep.tile([P, G], U8, name="d_scale_table", align_bytes=64)
         x_scale_table = keep.tile([P, T], U8, name="x_scale_table", align_bytes=64)
-        d_word_table = reused.tile([P, G], U32, name="d_word_table", offset=0, align_bytes=64)
-        x_word_table = reused.tile([P, T], U32, name="x_word_table", offset=4 * G, align_bytes=64)
+        d_word_table = keep.tile([P, G], U32, name="d_word_table", tag="d_words_then_x_plane", align_bytes=64)
         w_words_in = keep.tile([P, 2 * N], U8, name="w_words_in", tag="w_words_then_gains", align_bytes=64)
-        w_scales_in = reused.tile([P, N], U8, name="w_scales_in", offset=4 * G, align_bytes=64)
+        w_scales_in = keep.tile([P, N], U8, name="w_scales_in", tag="w_scales_then_x_words", align_bytes=64)
         d_plane = keep.tile([P, H], U8, name="d_plane", align_bytes=64)
 
         nc.vector.memset(d_scale_table[:].bitcast(I32), 0)
@@ -91,9 +89,6 @@ def tile_picked_scorepool_relu_po_kernel(
         def token_list(c):
             return offs_sb[:, c * CHUNK_J // LIST : (c + 1) * CHUNK_J // LIST]
 
-        def gather_x_scales(c):
-            nc.vector.tensor_copy(x_planes[c][:], x_scale_table[:].indirect(token_list(c)))
-
         def scores(c):
             nc.vector.tensor_copy(x_codes[c][:], x_word_table[:].indirect(token_list(c)))
             banks = []
@@ -107,7 +102,7 @@ def tile_picked_scorepool_relu_po_kernel(
                         lhsT=d_codes[:, keys].bitcast(FP8X4),
                         lhsT_scale=d_plane[:, keys],
                         rhs=x_codes[c][:, cols].bitcast(FP8X4),
-                        rhs_scale=x_planes[c][:, cols],
+                        rhs_scale=x_plane[:, c * CHUNK_J + b * BANK_J : c * CHUNK_J + (b + 1) * BANK_J],
                         start=True,
                         stop=True,
                     )
@@ -119,15 +114,14 @@ def tile_picked_scorepool_relu_po_kernel(
                 banks.append(bank)
             return banks
 
-        def pool(c, banks):
-            for b, bank in enumerate(banks):
-                rows = slice(b * BANK_V, (b + 1) * BANK_V)
-                nc.vector.tensor_tensor(
-                    pooled[c][:, rows, :],
-                    bank[:, :, 1:BANK_J:2].rearrange("p t v -> p v t"),
-                    firsts[c][:, rows, :],
-                    ALU.max,
-                )
+        def pool(c, b):
+            rows = slice(b * BANK_V, (b + 1) * BANK_V)
+            nc.vector.tensor_tensor(
+                pooled[c][:, rows, :],
+                score_banks[c][b][:, :, 1:BANK_J:2].rearrange("p t v -> p v t"),
+                firsts[c][:, rows, :],
+                ALU.max,
+            )
 
         def weigh(c):
             nc.vector.scalar_tensor_tensor(
@@ -169,11 +163,13 @@ def tile_picked_scorepool_relu_po_kernel(
                 low = out_psum.tile([P, 2, CHUNK_V], F32, name="out_bank")
                 product(low, 0, 2)
                 nc.scalar.copy(y_f32[c][:, 0:2, :], low[:])
-                nc.scalar.dma_start(out_rows[:, 0:2, cols], y_f32[c][:, 0:2, :])
+                nc.sync.dma_start(out_rows[:, 0:2, cols], y_f32[c][:, 0:2, :])
+                nc.scalar.copy(y_bf[c][:, :, 0:2], low[:].rearrange("p t v -> p v t"))
                 high = out_psum.tile([P, 2, CHUNK_V], F32, name="out_bank")
                 product(high, 2, 2)
+                nc.vector.tensor_copy(y_bf[c][:, :, 2:4], high[:].rearrange("p t v -> p v t"))
                 nc.vector.tensor_copy(y_f32[c][:, 2:4, :], high[:])
-                nc.sync.dma_start(out_rows[:, 2:4, cols], y_f32[c][:, 2:4, :])
+                nc.scalar.dma_start(out_rows[:, 2:4, cols], y_f32[c][:, 2:4, :])
 
         def round_out(c):
             nc.vector.tensor_copy(
@@ -189,6 +185,7 @@ def tile_picked_scorepool_relu_po_kernel(
         nc.vector.tensor_copy(
             w_scales_dealt[:].rearrange("p (t m) -> p t m", t=PACK), w_scales_in[:].rearrange("p (m t) -> p t m", t=PACK)
         )
+        x_word_table = keep.tile([P, T], U32, name="x_word_table", tag="w_scales_then_x_words", align_bytes=64)
         nc.sync.dma_start(x_word_table[:].bitcast(I32), x_words[0].rearrange("p c r -> p (c r)").bitcast(I32))
         nc.vector.tensor_copy(
             w_codes[:].rearrange("p (t m b) -> p t m b", t=PACK, b=2),
@@ -206,42 +203,34 @@ def tile_picked_scorepool_relu_po_kernel(
         nc.gpsimd.memset(w_plane[:].bitcast(I32), 0)
         to_plane(w_plane, w_scales_dealt, [nc.sync])
         nc.vector.tensor_copy(d_picked[:], d_word_table[:].indirect(kidx_sb[:]))
-        x_planes = [
-            reused.tile([P, CHUNK_J], U8, name="x_plane%d" % c, offset=c * CHUNK_J, align_bytes=64) for c in range(CHUNKS)
-        ]
-        gather_x_scales(0)
+        x_plane = keep.tile([P, S], U8, name="x_plane", tag="d_words_then_x_plane", align_bytes=64)
+        nc.vector.tensor_copy(x_plane[:], x_scale_table[:].indirect(offs_sb[:]))
         nc.vector.tensor_copy(
             d_codes[:].rearrange("p (t m) -> p m t", t=PACK), d_picked[:].rearrange("p (m t) -> p m t", t=PACK)
         )
-        banks0 = scores(0)
-        gather_x_scales(1)
-        banks1 = scores(1)
-        gather_x_scales(2)
-        banks2 = scores(2)
-        gather_x_scales(3)
-        pool(0, banks0)
-        weigh(0)
-        banks3 = scores(3)
-        values(0)
-        pool(1, banks1)
-        weigh(1)
-        pool(2, banks2)
-        values(1)
-        weigh(2)
-        pool(3, banks3)
-        values(2)
+        score_banks = [scores(c) for c in range(CHUNKS)]
+        words_out = out_1[0].rearrange("p c r -> p (c r)").bitcast(I32)
+
+        def store_words(first, stop):
+            cols = slice(first * CHUNK_V, stop * CHUNK_V)
+            nc.sync.dma_start(words_out[:, cols], y_codes[:, cols].bitcast(I32))
+
+        pool(0, 0)
+        pool(0, 1)
+        for c in range(CHUNKS - 1):
+            pool(c + 1, 0)
+            weigh(c)
+            pool(c + 1, 1)
+            values(c)
         quantise_out(0)
         weigh(3)
         quantise_out(1)
-        words_out = out_1[0].rearrange("p c r -> p (c r)").bitcast(I32)
-        early = V // 2
-        nc.sync.dma_start(words_out[:, 0:early], y_codes[:, 0:early].bitcast(I32))
+        store_words(0, 2)
         values(3)
         round_out(2)
         quantise_out(2)
-        round_out(3)
         quantise_out(3)
-        nc.sync.dma_start(words_out[:, early:V], y_codes[:, early:V].bitcast(I32))
+        store_words(2, 4)
         for q in range(4):
             queue = nc.scalar if q % 2 == 0 else nc.sync
             queue.dma_start(out_2[0, 4 * q : 4 * q + 4, :].bitcast(I32), y_plane[32 * q : 32 * q + 4, :].bitcast(I32))

@@ -36,60 +36,60 @@ def tile_picked_scorepool_relu_po_kernel(
         score_psum = ctx.enter_context(tc.psum_pool(name="score_psum", bufs=5))
         out_psum = ctx.enter_context(tc.psum_pool(name="out_psum", bufs=3))
 
+        def tile(shape, dtype, name, tag=""):
+            return keep.tile(shape, dtype, name=name, tag=tag or name, align_bytes=64)
+
         kidx_sb = keep.tile([P, H // LIST], U16, name="kidx_sb")
         offs_sb = keep.tile([P, S // LIST], U16, name="offs_sb")
-        d_scale_table = keep.tile([P, G], U8, name="d_scale_table", align_bytes=64)
-        x_scale_table = keep.tile([P, T], U8, name="x_scale_table", align_bytes=64)
-        d_word_table = keep.tile([P, G], U32, name="d_word_table", tag="d_words_then_x_plane", align_bytes=64)
-        w_words_in = keep.tile([P, 2 * N], U8, name="w_words_in", tag="w_words_then_gains", align_bytes=64)
-        w_scales_in = keep.tile([P, N], U8, name="w_scales_in", tag="w_scales_then_x_words", align_bytes=64)
-        d_plane = keep.tile([P, H], U8, name="d_plane", align_bytes=64)
+        d_scale_table = tile([P, G], U8, "d_scale_table")
+        x_word_table = tile([P, T], U32, "x_word_table")
+        x_scale_table = tile([P, T], U8, "x_scale_table")
+        w_scale_rows = tile([P, N], U8, "w_scale_rows")
+        d_word_table = tile([P, G], U32, "d_word_table")
+        w_words_in = tile([P, 2 * N], U8, "w_words_in")
+        gains = tile([P, PACK], F32, "gains")
 
-        nc.vector.memset(d_scale_table[:].bitcast(I32), 0)
         nc.vector.memset(x_scale_table[:].bitcast(I32), 0)
-        nc.vector.memset(d_plane[:].bitcast(I32), 0)
+        nc.vector.memset(d_scale_table[:].bitcast(I32), 0)
+        nc.gpsimd.memset(w_scale_rows[:].bitcast(I32), 0)
 
-        def by_block(scales):
-            rows = scales[0].bitcast(I32)
-            return rows.unsqueeze(1).to_broadcast([16, 8, rows.shape[1]])
-
-        def to_plane(plane, dealt, queues):
-            for r in range(4):
-                queues[r % len(queues)].dma_start(plane[r:P:32, :].bitcast(I32), dealt[8 * r : P : 32, :].bitcast(I32))
-
-        nc.sync.dma_start(w_scales_in[:].bitcast(I32), by_block(w1_scales))
-        for half in (slice(0, N), slice(N, 2 * N)):
-            nc.sync.dma_start(w_words_in[:, half].bitcast(I32), w1_words[0, :, half].bitcast(I32))
+        nc.scalar.dma_start(w_words_in[:].bitcast(I32), w1_words[0].bitcast(I32))
         nc.sync.dma_start(kidx_sb[:], kidx)
+        nc.scalar.dma_start(d_scale_table[0:P:8, :].bitcast(I32), d_scales[0].bitcast(I32))
         nc.sync.dma_start(offs_sb[:], offs)
-        nc.sync.dma_start(d_scale_table[0:P:8, :].bitcast(I32), d_scales[0].bitcast(I32))
+        for r in range(4):
+            nc.sync.dma_start(x_scale_table[r:P:32, :].bitcast(I32), x_scales[0, r:16:4, :].bitcast(I32))
         nc.sync.dma_start(d_word_table[:].bitcast(I32), d_words[0].rearrange("p c r -> p (c r)").bitcast(I32))
-        for q in range(4):
-            nc.sync.dma_start(
-                x_scale_table[32 * q : 32 * q + 4, :].bitcast(I32), x_scales[0, 4 * q : 4 * q + 4, :].bitcast(I32)
-            )
+        nc.sync.dma_start(w_scale_rows[0:P:8, :].bitcast(I32), w1_scales[0].bitcast(I32))
+        nc.sync.dma_start(x_word_table[:].bitcast(I32), x_words[0].rearrange("p c r -> p (c r)").bitcast(I32))
+        nc.sync.dma_start(gains[:], gn.rearrange("(p t) o -> p (t o)", t=PACK))
 
-        d_scales_picked = keep.tile([P, H], U8, name="d_scales_picked", tag="scale_bytes", align_bytes=64)
-        d_scales_dealt = keep.tile([P, H], U8, name="d_scales_dealt", align_bytes=64)
-        d_picked = keep.tile([P, H], U32, name="d_picked", align_bytes=64)
-        d_codes = keep.tile([P, H], U32, name="d_codes", align_bytes=64)
-        w_codes = keep.tile([P, 2 * N], U8, name="w_codes", align_bytes=64)
-        w_scales_dealt = keep.tile([P, N], U8, name="w_scales_dealt", align_bytes=64)
-        x_codes = [keep.tile([P, CHUNK_J], U32, name="x_codes%d" % c, align_bytes=64) for c in range(CHUNKS)]
-        firsts = [keep.tile([P, CHUNK_V, PACK], F32, name="first%d" % c) for c in range(CHUNKS)]
-        pooled = [keep.tile([P, CHUNK_V, PACK], F32, name="pooled%d" % c) for c in range(CHUNKS)]
-        z_bf = [keep.tile([P, CHUNK_V, PACK], BF16, name="z_bf%d" % c, align_bytes=64) for c in range(CHUNKS)]
-        z_codes = [keep.tile([P, CHUNK_V], U32, name="z_codes%d" % c, align_bytes=64) for c in range(CHUNKS)]
-        z_planes = [keep.tile([P, CHUNK_V], U8, name="z_plane%d" % c, align_bytes=64) for c in range(CHUNKS)]
-        y_f32 = [keep.tile([P, PACK, CHUNK_V], F32, name="y_f32_%d" % c) for c in range(CHUNKS)]
-        y_bf = [keep.tile([P, CHUNK_V, PACK], BF16, name="y_bf%d" % c, align_bytes=64) for c in range(CHUNKS)]
-        y_codes = keep.tile([P, V], U32, name="y_codes", align_bytes=64)
-        y_plane = keep.tile([P, V], U8, name="y_plane", align_bytes=64)
+        d_scales_picked = tile([P, H], U8, "d_scales_picked")
+        d_plane = tile([P, H], U8, "d_plane")
+        d_picked = tile([P, H], U32, "d_picked")
+        d_codes = tile([P, H], U32, "d_codes")
+        w_codes = tile([P, 2 * N], U8, "w_codes")
+        x_codes, x_planes, firsts = {}, {}, {}
+        pooled = [tile([P, CHUNK_V, PACK], F32, "pooled%d" % c) for c in range(CHUNKS)]
+        z_bf = [tile([P, CHUNK_V, PACK], BF16, "z_bf%d" % c) for c in range(CHUNKS)]
+        z_codes = [tile([P, CHUNK_V], U32, "z_codes%d" % c) for c in range(CHUNKS)]
+        z_planes = [tile([P, CHUNK_V], U8, "z_plane%d" % c) for c in range(CHUNKS)]
+        y_f32 = [tile([P, PACK, CHUNK_V], F32, "y_f32_%d" % c) for c in range(CHUNKS)]
+        y_bf = [tile([P, CHUNK_V, PACK], BF16, "y_bf%d" % c) for c in range(CHUNKS)]
+        y_codes = tile([P, V], U32, "y_codes")
+        y_plane = tile([P, V], U8, "y_plane")
+        out_rows = out_0.rearrange("(p t) v -> p t v", t=PACK)
+        words_out = out_1[0].rearrange("p c r -> p (c r)").bitcast(I32)
+
+        def to_plane(plane, queue):
+            for r in range(1, 4):
+                queue.dma_start(plane[r:P:32, :].bitcast(I32), plane[8 * r : P : 32, :].bitcast(I32))
 
         def token_list(c):
             return offs_sb[:, c * CHUNK_J // LIST : (c + 1) * CHUNK_J // LIST]
 
-        def scores(c):
+        def scores(c, tag=""):
+            x_codes[c] = tile([P, CHUNK_J], U32, "x_codes%d" % c, tag)
             nc.vector.tensor_copy(x_codes[c][:], x_word_table[:].indirect(token_list(c)))
             banks = []
             for b in range(CHUNK_J // BANK_J):
@@ -106,75 +106,67 @@ def tile_picked_scorepool_relu_po_kernel(
                         start=True,
                         stop=True,
                     )
+                firsts[c, b] = tile([P, BANK_V, PACK], F32, "first%d_%d" % (c, b))
                 nc.scalar.activation(
-                    firsts[c][:, b * BANK_V : (b + 1) * BANK_V, :],
+                    firsts[c, b][:],
                     bank[:, :, 0:BANK_J:2].rearrange("p t v -> p v t"),
                     ACT.Relu,
+                    scale=SCORE_SCALE,
                 )
                 banks.append(bank)
             return banks
 
         def pool(c, b):
             rows = slice(b * BANK_V, (b + 1) * BANK_V)
-            nc.vector.tensor_tensor(
+            nc.vector.scalar_tensor_tensor(
                 pooled[c][:, rows, :],
                 score_banks[c][b][:, :, 1:BANK_J:2].rearrange("p t v -> p v t"),
-                firsts[c][:, rows, :],
+                SCORE_SCALE,
+                firsts[c, b][:],
+                ALU.mult,
                 ALU.max,
             )
 
         def weigh(c):
-            nc.vector.scalar_tensor_tensor(
-                z_bf[c][:],
-                pooled[c][:],
-                SCORE_SCALE,
-                gains[:].unsqueeze(1).to_broadcast([P, CHUNK_V, PACK]),
-                ALU.mult,
-                ALU.mult,
+            engine = nc.vector
+            engine.tensor_tensor(
+                z_bf[c][:], pooled[c][:], gains[:].unsqueeze(1).to_broadcast([P, CHUNK_V, PACK]), ALU.mult
             )
+
+        def product(c, bank, first, count):
+            for t in range(first, first + count):
+                nc.tensor.matmul_mx(
+                    out=bank[:, t - first, :],
+                    lhsT=w_codes[:, 2 * t * P : 2 * (t + 1) * P].bitcast(FP4X4),
+                    lhsT_scale=w_plane[:, t * P : (t + 1) * P],
+                    rhs=z_codes[c][:].bitcast(FP8X4),
+                    rhs_scale=z_planes[c][:],
+                    start=True,
+                    stop=True,
+                )
 
         def values(c):
             nc.vector.quantize_mx(
                 out=z_codes[c][:].bitcast(FP8X4), scales=z_planes[c][:], in_=z_bf[c][:].rearrange("p v t -> p (v t)")
             )
             cols = slice(c * CHUNK_V, (c + 1) * CHUNK_V)
-            out_rows = out_0.rearrange("(p t) v -> p t v", t=PACK)
-
-            def product(bank, first, count):
-                for t in range(first, first + count):
-                    nc.tensor.matmul_mx(
-                        out=bank[:, t - first, :],
-                        lhsT=w_codes[:, 2 * t * P : 2 * (t + 1) * P].bitcast(FP4X4),
-                        lhsT_scale=w_plane[:, t * P : (t + 1) * P],
-                        rhs=z_codes[c][:].bitcast(FP8X4),
-                        rhs_scale=z_planes[c][:],
-                        start=True,
-                        stop=True,
-                    )
-
             if c < CHUNKS - 1:
                 bank = out_psum.tile([P, PACK, CHUNK_V], F32, name="out_bank")
-                product(bank, 0, PACK)
-                if c < CHUNKS - 2:
-                    nc.scalar.copy(y_bf[c][:], bank[:].rearrange("p t v -> p v t"))
+                product(c, bank, 0, PACK)
                 nc.scalar.copy(y_f32[c][:], bank[:])
                 nc.sync.dma_start(out_rows[:, :, cols], y_f32[c][:])
+                nc.scalar.copy(y_bf[c][:], bank[:].rearrange("p t v -> p v t"))
             else:
                 low = out_psum.tile([P, 2, CHUNK_V], F32, name="out_bank")
-                product(low, 0, 2)
+                product(c, low, 0, 2)
                 nc.scalar.copy(y_f32[c][:, 0:2, :], low[:])
                 nc.sync.dma_start(out_rows[:, 0:2, cols], y_f32[c][:, 0:2, :])
                 nc.scalar.copy(y_bf[c][:, :, 0:2], low[:].rearrange("p t v -> p v t"))
                 high = out_psum.tile([P, 2, CHUNK_V], F32, name="out_bank")
-                product(high, 2, 2)
+                product(c, high, 2, 2)
                 nc.vector.tensor_copy(y_bf[c][:, :, 2:4], high[:].rearrange("p t v -> p v t"))
                 nc.vector.tensor_copy(y_f32[c][:, 2:4, :], high[:])
                 nc.scalar.dma_start(out_rows[:, 2:4, cols], y_f32[c][:, 2:4, :])
-
-        def round_out(c):
-            nc.vector.tensor_copy(
-                y_bf[c][:].rearrange("p (u i) t -> p u t i", i=4), y_f32[c][:].rearrange("p t (u i) -> p u t i", i=4)
-            )
 
         def quantise_out(c):
             cols = slice(c * CHUNK_V, (c + 1) * CHUNK_V)
@@ -182,39 +174,36 @@ def tile_picked_scorepool_relu_po_kernel(
                 out=y_codes[:, cols].bitcast(FP8X4), scales=y_plane[:, cols], in_=y_bf[c][:].rearrange("p v t -> p (v t)")
             )
 
-        nc.vector.tensor_copy(
-            w_scales_dealt[:].rearrange("p (t m) -> p t m", t=PACK), w_scales_in[:].rearrange("p (m t) -> p t m", t=PACK)
-        )
-        x_word_table = keep.tile([P, T], U32, name="x_word_table", tag="w_scales_then_x_words", align_bytes=64)
-        nc.sync.dma_start(x_word_table[:].bitcast(I32), x_words[0].rearrange("p c r -> p (c r)").bitcast(I32))
-        nc.vector.tensor_copy(
-            w_codes[:].rearrange("p (t m b) -> p t m b", t=PACK, b=2),
-            w_words_in[:].rearrange("p (m t b) -> p t m b", t=PACK, b=2),
-        )
-        gains = keep.tile([P, PACK], F32, name="gains", tag="w_words_then_gains", align_bytes=64)
-        nc.sync.dma_start(gains[:], gn.rearrange("(p t) o -> p (t o)", t=PACK))
-        nc.vector.tensor_copy(d_scales_picked[:], d_scale_table[:].indirect(kidx_sb[:]))
-        nc.vector.tensor_copy(
-            d_scales_dealt[:].rearrange("p (t m) -> p t m", t=PACK),
-            d_scales_picked[:].rearrange("p (m t) -> p t m", t=PACK),
-        )
-        to_plane(d_plane, d_scales_dealt, [nc.scalar])
-        w_plane = keep.tile([P, N], U8, name="w_plane", tag="scale_bytes", align_bytes=64)
-        nc.gpsimd.memset(w_plane[:].bitcast(I32), 0)
-        to_plane(w_plane, w_scales_dealt, [nc.sync])
-        nc.vector.tensor_copy(d_picked[:], d_word_table[:].indirect(kidx_sb[:]))
-        x_plane = keep.tile([P, S], U8, name="x_plane", tag="d_words_then_x_plane", align_bytes=64)
-        nc.vector.tensor_copy(x_plane[:], x_scale_table[:].indirect(offs_sb[:]))
-        nc.vector.tensor_copy(
-            d_codes[:].rearrange("p (t m) -> p m t", t=PACK), d_picked[:].rearrange("p (m t) -> p m t", t=PACK)
-        )
-        score_banks = [scores(c) for c in range(CHUNKS)]
-        words_out = out_1[0].rearrange("p c r -> p (c r)").bitcast(I32)
-
         def store_words(first, stop):
             cols = slice(first * CHUNK_V, stop * CHUNK_V)
             nc.sync.dma_start(words_out[:, cols], y_codes[:, cols].bitcast(I32))
 
+        nc.vector.tensor_copy(
+            w_codes[:].rearrange("p (t m b) -> p t m b", t=PACK, b=2),
+            w_words_in[:].rearrange("p (m t b) -> p t m b", t=PACK, b=2),
+        )
+        key_halves = [slice(h * H // 2, (h + 1) * H // 2) for h in range(2)]
+        key_lists = [kidx_sb[:, keys.start // LIST : keys.stop // LIST] for keys in key_halves]
+        for keys, entries in zip(key_halves, key_lists):
+            nc.vector.tensor_copy(d_scales_picked[:, keys], d_scale_table[:].indirect(entries))
+        for keys in key_halves:
+            nc.vector.tensor_copy(
+                d_plane[:].rearrange("p (t m) -> p t m", t=PACK)[:, :, keys.start // PACK : keys.stop // PACK],
+                d_scales_picked[:, keys].rearrange("p (m t) -> p t m", t=PACK),
+            )
+        to_plane(d_plane, nc.scalar)
+        x_plane = tile([P, S], U8, "x_plane")
+        nc.vector.tensor_copy(x_plane[:], x_scale_table[:].indirect(offs_sb[:]))
+        nc.vector.tensor_copy(d_picked[:], d_word_table[:].indirect(kidx_sb[:]))
+        w_plane = tile([P, N], U8, "w_plane")
+        nc.vector.tensor_copy(
+            w_plane[:].rearrange("p (t m) -> p t m", t=PACK), w_scale_rows[:].rearrange("p (m t) -> p t m", t=PACK)
+        )
+        nc.vector.tensor_copy(
+            d_codes[:].rearrange("p (t m) -> p m t", t=PACK), d_picked[:].rearrange("p (m t) -> p m t", t=PACK)
+        )
+        to_plane(w_plane, nc.sync)
+        score_banks = [scores(c) for c in range(CHUNKS)]
         pool(0, 0)
         pool(0, 1)
         for c in range(CHUNKS - 1):
@@ -227,7 +216,6 @@ def tile_picked_scorepool_relu_po_kernel(
         quantise_out(1)
         store_words(0, 2)
         values(3)
-        round_out(2)
         quantise_out(2)
         quantise_out(3)
         store_words(2, 4)

@@ -49,12 +49,13 @@ def tile_picked_scorepool_relu_po_kernel(
         w_words_in = tile([P, 2 * N], U8, "w_words_in")
         gains = tile([P, PACK], F32, "gains")
 
-        nc.vector.memset(x_scale_table[:].bitcast(I32), 0)
         nc.vector.memset(d_scale_table[:].bitcast(I32), 0)
+        nc.vector.memset(x_scale_table[:, : 3 * T // 4].bitcast(I32), 0)
+        nc.gpsimd.memset(x_scale_table[:, 3 * T // 4 :].bitcast(I32), 0)
         nc.gpsimd.memset(w_scale_rows[:].bitcast(I32), 0)
 
-        nc.scalar.dma_start(w_words_in[:].bitcast(I32), w1_words[0].bitcast(I32))
         nc.sync.dma_start(kidx_sb[:], kidx)
+        nc.scalar.dma_start(w_words_in[:].bitcast(I32), w1_words[0].bitcast(I32))
         nc.scalar.dma_start(d_scale_table[0:P:8, :].bitcast(I32), d_scales[0].bitcast(I32))
         nc.sync.dma_start(offs_sb[:], offs)
         for r in range(4):
@@ -85,12 +86,14 @@ def tile_picked_scorepool_relu_po_kernel(
             for r in range(1, 4):
                 queue.dma_start(plane[r:P:32, :].bitcast(I32), plane[8 * r : P : 32, :].bitcast(I32))
 
-        def token_list(c):
-            return offs_sb[:, c * CHUNK_J // LIST : (c + 1) * CHUNK_J // LIST]
+        def pick_words(first, stop):
+            picked = tile([P, (stop - first) * CHUNK_J], U32, "x_codes%d" % first)
+            entries = offs_sb[:, first * CHUNK_J // LIST : stop * CHUNK_J // LIST]
+            nc.vector.tensor_copy(picked[:], x_word_table[:].indirect(entries))
+            for c in range(first, stop):
+                x_codes[c] = picked[:, (c - first) * CHUNK_J : (c - first + 1) * CHUNK_J]
 
-        def scores(c, tag=""):
-            x_codes[c] = tile([P, CHUNK_J], U32, "x_codes%d" % c, tag)
-            nc.vector.tensor_copy(x_codes[c][:], x_word_table[:].indirect(token_list(c)))
+        def scores(c):
             banks = []
             for b in range(CHUNK_J // BANK_J):
                 bank = score_psum.tile([P, PACK, BANK_J], F32, name="score_bank")
@@ -203,7 +206,10 @@ def tile_picked_scorepool_relu_po_kernel(
             d_codes[:].rearrange("p (t m) -> p m t", t=PACK), d_picked[:].rearrange("p (m t) -> p m t", t=PACK)
         )
         to_plane(w_plane, nc.sync)
-        score_banks = [scores(c) for c in range(CHUNKS)]
+        score_banks = []
+        for first, stop in ((0, 1), (1, 2), (2, 4)):
+            pick_words(first, stop)
+            score_banks.extend(scores(c) for c in range(first, stop))
         pool(0, 0)
         pool(0, 1)
         for c in range(CHUNKS - 1):

@@ -50,20 +50,19 @@ def tile_picked_scorepool_relu_po_kernel(
         gains = tile([P, PACK], F32, "gains")
 
         nc.vector.memset(d_scale_table[:].bitcast(I32), 0)
-        nc.vector.memset(x_scale_table[:, : 3 * T // 4].bitcast(I32), 0)
-        nc.gpsimd.memset(x_scale_table[:, 3 * T // 4 :].bitcast(I32), 0)
-        nc.gpsimd.memset(w_scale_rows[:].bitcast(I32), 0)
+        nc.vector.memset(x_scale_table[:].bitcast(I32), 0)
+        nc.vector.memset(w_scale_rows[:].bitcast(I32), 0)
 
         nc.sync.dma_start(kidx_sb[:], kidx)
-        nc.scalar.dma_start(w_words_in[:].bitcast(I32), w1_words[0].bitcast(I32))
-        nc.scalar.dma_start(d_scale_table[0:P:8, :].bitcast(I32), d_scales[0].bitcast(I32))
+        nc.sync.dma_start(d_scale_table[0:P:8, :].bitcast(I32), d_scales[0].bitcast(I32))
         nc.sync.dma_start(offs_sb[:], offs)
         for r in range(4):
-            nc.sync.dma_start(x_scale_table[r:P:32, :].bitcast(I32), x_scales[0, r:16:4, :].bitcast(I32))
+            nc.scalar.dma_start(x_scale_table[r:P:32, :].bitcast(I32), x_scales[0, r:16:4, :].bitcast(I32))
         nc.sync.dma_start(d_word_table[:].bitcast(I32), d_words[0].rearrange("p c r -> p (c r)").bitcast(I32))
-        nc.sync.dma_start(w_scale_rows[0:P:8, :].bitcast(I32), w1_scales[0].bitcast(I32))
         nc.sync.dma_start(x_word_table[:].bitcast(I32), x_words[0].rearrange("p c r -> p (c r)").bitcast(I32))
-        nc.sync.dma_start(gains[:], gn.rearrange("(p t) o -> p (t o)", t=PACK))
+        nc.scalar.dma_start(w_scale_rows[0:P:8, :].bitcast(I32), w1_scales[0].bitcast(I32))
+        nc.scalar.dma_start(gains[:], gn.rearrange("(p t) o -> p (t o)", t=PACK))
+        nc.sync.dma_start(w_words_in[:].bitcast(I32), w1_words[0].bitcast(I32))
 
         d_scales_picked = tile([P, H], U8, "d_scales_picked")
         d_plane = tile([P, H], U8, "d_plane")
@@ -181,10 +180,6 @@ def tile_picked_scorepool_relu_po_kernel(
             cols = slice(first * CHUNK_V, stop * CHUNK_V)
             nc.sync.dma_start(words_out[:, cols], y_codes[:, cols].bitcast(I32))
 
-        nc.vector.tensor_copy(
-            w_codes[:].rearrange("p (t m b) -> p t m b", t=PACK, b=2),
-            w_words_in[:].rearrange("p (m t b) -> p t m b", t=PACK, b=2),
-        )
         key_halves = [slice(h * H // 2, (h + 1) * H // 2) for h in range(2)]
         key_lists = [kidx_sb[:, keys.start // LIST : keys.stop // LIST] for keys in key_halves]
         for keys, entries in zip(key_halves, key_lists):
@@ -199,8 +194,12 @@ def tile_picked_scorepool_relu_po_kernel(
         nc.vector.tensor_copy(x_plane[:], x_scale_table[:].indirect(offs_sb[:]))
         nc.vector.tensor_copy(d_picked[:], d_word_table[:].indirect(kidx_sb[:]))
         w_plane = tile([P, N], U8, "w_plane")
-        nc.vector.tensor_copy(
+        nc.gpsimd.tensor_copy(
             w_plane[:].rearrange("p (t m) -> p t m", t=PACK), w_scale_rows[:].rearrange("p (m t) -> p t m", t=PACK)
+        )
+        nc.scalar.copy(
+            w_codes[:].bitcast(U16).rearrange("p (t m) -> p t m", t=PACK),
+            w_words_in[:].bitcast(U16).rearrange("p (m t) -> p t m", t=PACK),
         )
         nc.vector.tensor_copy(
             d_codes[:].rearrange("p (t m) -> p m t", t=PACK), d_picked[:].rearrange("p (m t) -> p m t", t=PACK)

@@ -50,19 +50,19 @@ def tile_picked_scorepool_relu_po_kernel(
         gains = tile([P, PACK], F32, "gains")
 
         nc.vector.memset(d_scale_table[:].bitcast(I32), 0)
-        nc.vector.memset(x_scale_table[:].bitcast(I32), 0)
         nc.vector.memset(w_scale_rows[:].bitcast(I32), 0)
+        nc.vector.memset(x_scale_table[:].bitcast(I32), 0)
 
         nc.sync.dma_start(kidx_sb[:], kidx)
         nc.sync.dma_start(d_scale_table[0:P:8, :].bitcast(I32), d_scales[0].bitcast(I32))
         nc.sync.dma_start(offs_sb[:], offs)
-        for r in range(4):
-            nc.scalar.dma_start(x_scale_table[r:P:32, :].bitcast(I32), x_scales[0, r:16:4, :].bitcast(I32))
+        nc.sync.dma_start(w_scale_rows[0:P:8, :].bitcast(I32), w1_scales[0].bitcast(I32))
         nc.sync.dma_start(d_word_table[:].bitcast(I32), d_words[0].rearrange("p c r -> p (c r)").bitcast(I32))
+        for r in range(4):
+            nc.sync.dma_start(x_scale_table[r:P:32, :].bitcast(I32), x_scales[0, r:16:4, :].bitcast(I32))
         nc.sync.dma_start(x_word_table[:].bitcast(I32), x_words[0].rearrange("p c r -> p (c r)").bitcast(I32))
-        nc.scalar.dma_start(w_scale_rows[0:P:8, :].bitcast(I32), w1_scales[0].bitcast(I32))
-        nc.scalar.dma_start(gains[:], gn.rearrange("(p t) o -> p (t o)", t=PACK))
         nc.sync.dma_start(w_words_in[:].bitcast(I32), w1_words[0].bitcast(I32))
+        nc.sync.dma_start(gains[:], gn.rearrange("(p t) o -> p (t o)", t=PACK))
 
         d_scales_picked = tile([P, H], U8, "d_scales_picked")
         d_plane = tile([P, H], U8, "d_plane")
@@ -191,8 +191,8 @@ def tile_picked_scorepool_relu_po_kernel(
             )
         to_plane(d_plane, nc.scalar)
         x_plane = tile([P, S], U8, "x_plane")
-        nc.vector.tensor_copy(x_plane[:], x_scale_table[:].indirect(offs_sb[:]))
-        nc.vector.tensor_copy(d_picked[:], d_word_table[:].indirect(kidx_sb[:]))
+        for keys, entries in zip(key_halves, key_lists):
+            nc.vector.tensor_copy(d_picked[:, keys], d_word_table[:].indirect(entries))
         w_plane = tile([P, N], U8, "w_plane")
         nc.gpsimd.tensor_copy(
             w_plane[:].rearrange("p (t m) -> p t m", t=PACK), w_scale_rows[:].rearrange("p (m t) -> p t m", t=PACK)
@@ -201,9 +201,12 @@ def tile_picked_scorepool_relu_po_kernel(
             w_codes[:].bitcast(U16).rearrange("p (t m) -> p t m", t=PACK),
             w_words_in[:].bitcast(U16).rearrange("p (m t) -> p t m", t=PACK),
         )
-        nc.vector.tensor_copy(
-            d_codes[:].rearrange("p (t m) -> p m t", t=PACK), d_picked[:].rearrange("p (m t) -> p m t", t=PACK)
-        )
+        for keys in key_halves:
+            nc.vector.tensor_copy(
+                d_codes[:].rearrange("p (t m) -> p m t", t=PACK)[:, keys.start // PACK : keys.stop // PACK, :],
+                d_picked[:, keys].rearrange("p (m t) -> p m t", t=PACK),
+            )
+        nc.vector.tensor_copy(x_plane[:], x_scale_table[:].indirect(offs_sb[:]))
         to_plane(w_plane, nc.sync)
         score_banks = []
         for first, stop in ((0, 1), (1, 2), (2, 4)):

@@ -49,20 +49,19 @@ def tile_picked_scorepool_relu_po_kernel(
         w_words_in = tile([P, 2 * N], U8, "w_words_in")
         gains = tile([P, PACK], F32, "gains")
 
+        x_plane = tile([P, S], U8, "x_plane")
         nc.vector.memset(d_scale_table[:].bitcast(I32), 0)
-        nc.vector.memset(w_scale_rows[:].bitcast(I32), 0)
         nc.vector.memset(x_scale_table[:].bitcast(I32), 0)
+        nc.vector.memset(w_scale_rows[:].bitcast(I32), 0)
+        nc.vector.memset(x_plane[:].bitcast(I32), 0)
 
         nc.sync.dma_start(kidx_sb[:], kidx)
         nc.sync.dma_start(d_scale_table[0:P:8, :].bitcast(I32), d_scales[0].bitcast(I32))
         nc.sync.dma_start(offs_sb[:], offs)
         nc.sync.dma_start(w_scale_rows[0:P:8, :].bitcast(I32), w1_scales[0].bitcast(I32))
+        nc.scalar.dma_start(x_scale_table[0:P:8, :].bitcast(I32), x_scales[0].bitcast(I32))
         nc.sync.dma_start(d_word_table[:].bitcast(I32), d_words[0].rearrange("p c r -> p (c r)").bitcast(I32))
-        for r in range(4):
-            nc.sync.dma_start(x_scale_table[r:P:32, :].bitcast(I32), x_scales[0, r:16:4, :].bitcast(I32))
         nc.sync.dma_start(x_word_table[:].bitcast(I32), x_words[0].rearrange("p c r -> p (c r)").bitcast(I32))
-        nc.sync.dma_start(w_words_in[:].bitcast(I32), w1_words[0].bitcast(I32))
-        nc.sync.dma_start(gains[:], gn.rearrange("(p t) o -> p (t o)", t=PACK))
 
         d_scales_picked = tile([P, H], U8, "d_scales_picked")
         d_plane = tile([P, H], U8, "d_plane")
@@ -182,22 +181,25 @@ def tile_picked_scorepool_relu_po_kernel(
 
         key_halves = [slice(h * H // 2, (h + 1) * H // 2) for h in range(2)]
         key_lists = [kidx_sb[:, keys.start // LIST : keys.stop // LIST] for keys in key_halves]
-        for keys, entries in zip(key_halves, key_lists):
-            nc.vector.tensor_copy(d_scales_picked[:, keys], d_scale_table[:].indirect(entries))
-        for keys in key_halves:
-            nc.vector.tensor_copy(
-                d_plane[:].rearrange("p (t m) -> p t m", t=PACK)[:, :, keys.start // PACK : keys.stop // PACK],
-                d_scales_picked[:, keys].rearrange("p (m t) -> p t m", t=PACK),
-            )
+        x_scales_picked = tile([P, S], U8, "x_scales_picked")
+        nc.vector.tensor_copy(d_scales_picked[:], d_scale_table[:].indirect(kidx_sb[:]))
+        nc.vector.tensor_copy(x_scales_picked[:, : S // 2], x_scale_table[:].indirect(offs_sb[:, : S // 2 // LIST]))
+        nc.vector.tensor_copy(
+            d_plane[:].rearrange("p (t m) -> p t m", t=PACK), d_scales_picked[:].rearrange("p (m t) -> p t m", t=PACK)
+        )
+        nc.vector.tensor_copy(x_scales_picked[:, S // 2 :], x_scale_table[:].indirect(offs_sb[:, S // 2 // LIST :]))
         to_plane(d_plane, nc.scalar)
-        x_plane = tile([P, S], U8, "x_plane")
+        for r in range(4):
+            nc.sync.dma_start(x_plane[r:P:32, :].bitcast(I32), x_scales_picked[8 * r : P : 32, :].bitcast(I32))
+        nc.sync.dma_start(w_words_in[:].bitcast(I32), w1_words[0].bitcast(I32))
+        nc.sync.dma_start(gains[:], gn.rearrange("(p t) o -> p (t o)", t=PACK))
         for keys, entries in zip(key_halves, key_lists):
             nc.vector.tensor_copy(d_picked[:, keys], d_word_table[:].indirect(entries))
         w_plane = tile([P, N], U8, "w_plane")
         nc.gpsimd.tensor_copy(
             w_plane[:].rearrange("p (t m) -> p t m", t=PACK), w_scale_rows[:].rearrange("p (m t) -> p t m", t=PACK)
         )
-        nc.scalar.copy(
+        nc.gpsimd.tensor_copy(
             w_codes[:].bitcast(U16).rearrange("p (t m) -> p t m", t=PACK),
             w_words_in[:].bitcast(U16).rearrange("p (m t) -> p t m", t=PACK),
         )
@@ -206,7 +208,6 @@ def tile_picked_scorepool_relu_po_kernel(
                 d_codes[:].rearrange("p (t m) -> p m t", t=PACK)[:, keys.start // PACK : keys.stop // PACK, :],
                 d_picked[:, keys].rearrange("p (m t) -> p m t", t=PACK),
             )
-        nc.vector.tensor_copy(x_plane[:], x_scale_table[:].indirect(offs_sb[:]))
         to_plane(w_plane, nc.sync)
         score_banks = []
         for first, stop in ((0, 1), (1, 2), (2, 4)):

@@ -67,7 +67,6 @@ def tile_picked_scorepool_relu_po_kernel(
         d_plane = tile([P, H], U8, "d_plane")
         d_picked = tile([P, H], U32, "d_picked")
         d_codes = tile([P, H], U32, "d_codes")
-        w_codes = tile([P, 2 * N], U8, "w_codes")
         x_codes, x_planes, firsts = {}, {}, {}
         pooled = [tile([P, CHUNK_V, PACK], F32, "pooled%d" % c) for c in range(CHUNKS)]
         z_bf = [tile([P, CHUNK_V, PACK], BF16, "z_bf%d" % c) for c in range(CHUNKS)]
@@ -191,17 +190,13 @@ def tile_picked_scorepool_relu_po_kernel(
         to_plane(d_plane, nc.scalar)
         for r in range(4):
             nc.sync.dma_start(x_plane[r:P:32, :].bitcast(I32), x_scales_picked[8 * r : P : 32, :].bitcast(I32))
-        nc.sync.dma_start(w_words_in[:].bitcast(I32), w1_words[0].bitcast(I32))
         nc.sync.dma_start(gains[:], gn.rearrange("(p t) o -> p (t o)", t=PACK))
+        nc.sync.dma_start(w_words_in[:].bitcast(I32), w1_words[0].bitcast(I32))
         for keys, entries in zip(key_halves, key_lists):
             nc.vector.tensor_copy(d_picked[:, keys], d_word_table[:].indirect(entries))
         w_plane = tile([P, N], U8, "w_plane")
         nc.gpsimd.tensor_copy(
             w_plane[:].rearrange("p (t m) -> p t m", t=PACK), w_scale_rows[:].rearrange("p (m t) -> p t m", t=PACK)
-        )
-        nc.gpsimd.tensor_copy(
-            w_codes[:].bitcast(U16).rearrange("p (t m) -> p t m", t=PACK),
-            w_words_in[:].bitcast(U16).rearrange("p (m t) -> p t m", t=PACK),
         )
         for keys in key_halves:
             nc.vector.tensor_copy(
@@ -210,9 +205,16 @@ def tile_picked_scorepool_relu_po_kernel(
             )
         to_plane(w_plane, nc.sync)
         score_banks = []
-        for first, stop in ((0, 1), (1, 2), (2, 4)):
-            pick_words(first, stop)
-            score_banks.extend(scores(c) for c in range(first, stop))
+        for c in range(2):
+            pick_words(c, c + 1)
+            score_banks.append(scores(c))
+        w_codes = tile([P, 2 * N], U8, "w_codes", "x_codes1")
+        nc.scalar.copy(
+            w_codes[:].bitcast(U16).rearrange("p (t m) -> p t m", t=PACK),
+            w_words_in[:].bitcast(U16).rearrange("p (m t) -> p t m", t=PACK),
+        )
+        pick_words(2, 4)
+        score_banks.extend(scores(c) for c in range(2, 4))
         pool(0, 0)
         pool(0, 1)
         for c in range(CHUNKS - 1):

@@ -1,6 +1,7 @@
 from contextlib import ExitStack
 
 import concourse.mybir as mybir
+from concourse.masks import make_identity
 
 K, T, S, V, N, G, H = 512, 2048, 1024, 512, 512, 2048, 512
 FLOPS = 2 * K * H * S + 2 * H * N * V
@@ -25,6 +26,8 @@ CHUNK_J = 2 * CHUNK_V
 CHUNKS = V // CHUNK_V
 BANK_J = 128
 BANK_V = BANK_J // 2
+POOL_V = 32
+TURN_V = P // PACK
 
 
 def tile_picked_scorepool_relu_po_kernel(
@@ -33,8 +36,9 @@ def tile_picked_scorepool_relu_po_kernel(
     nc = tc.nc
     with ExitStack() as ctx:
         keep = ctx.enter_context(tc.tile_pool(name="keep", bufs=1))
-        score_psum = ctx.enter_context(tc.psum_pool(name="score_psum", bufs=5))
-        out_psum = ctx.enter_context(tc.psum_pool(name="out_psum", bufs=3))
+        last = ctx.enter_context(tc.tile_pool(name="last", bufs=1))
+        gain_psum = ctx.enter_context(tc.psum_pool(name="gain_psum", bufs=1))
+        psum = ctx.enter_context(tc.psum_pool(name="psum", bufs=7))
 
         def tile(shape, dtype, name, tag=""):
             return keep.tile(shape, dtype, name=name, tag=tag or name, align_bytes=64)
@@ -47,19 +51,25 @@ def tile_picked_scorepool_relu_po_kernel(
         w_scale_rows = tile([P, N], U8, "w_scale_rows")
         d_word_table = tile([P, G], U32, "d_word_table")
         w_words_in = tile([P, 2 * N], U8, "w_words_in")
-        gains = tile([P, PACK], F32, "gains")
+        gain_cols = tile([P, PACK], F32, "gain_cols")
+        gains = tile([P, POOL_V, PACK], F32, "gains")
+        gains_turned = tile([P, P], F32, "gains_turned")
+        identity = tile([P, P], F32, "identity")
 
         x_plane = tile([P, S], U8, "x_plane")
         nc.vector.memset(d_scale_table[:].bitcast(I32), 0)
         nc.vector.memset(x_scale_table[:].bitcast(I32), 0)
         nc.vector.memset(w_scale_rows[:].bitcast(I32), 0)
         nc.vector.memset(x_plane[:].bitcast(I32), 0)
+        nc.vector.memset(identity[:], 0.0)
+        make_identity(nc, identity[:], nomemset=True)
 
         nc.sync.dma_start(kidx_sb[:], kidx)
         nc.sync.dma_start(d_scale_table[0:P:8, :].bitcast(I32), d_scales[0].bitcast(I32))
         nc.sync.dma_start(offs_sb[:], offs)
         nc.sync.dma_start(w_scale_rows[0:P:8, :].bitcast(I32), w1_scales[0].bitcast(I32))
         nc.scalar.dma_start(x_scale_table[0:P:8, :].bitcast(I32), x_scales[0].bitcast(I32))
+        nc.scalar.dma_start(gain_cols[:], gn.rearrange("(p t) o -> p (t o)", t=PACK))
         nc.sync.dma_start(d_word_table[:].bitcast(I32), d_words[0].rearrange("p c r -> p (c r)").bitcast(I32))
         nc.sync.dma_start(x_word_table[:].bitcast(I32), x_words[0].rearrange("p c r -> p (c r)").bitcast(I32))
 
@@ -68,13 +78,14 @@ def tile_picked_scorepool_relu_po_kernel(
         d_picked = tile([P, H], U32, "d_picked")
         d_codes = tile([P, H], U32, "d_codes")
         x_codes, x_planes, firsts = {}, {}, {}
-        pooled = [tile([P, CHUNK_V, PACK], F32, "pooled%d" % c) for c in range(CHUNKS)]
-        z_bf = [tile([P, CHUNK_V, PACK], BF16, "z_bf%d" % c) for c in range(CHUNKS)]
+        pooled = {}
+        z_bf = [tile([P, CHUNK_V, PACK], BF16, "z_bf%d" % c) for c in range(CHUNKS - 1)]
+        z_bf.append(last.tile([P, CHUNK_V, PACK], BF16, name="z_bf3", align_bytes=64, offset=512))
         z_codes = [tile([P, CHUNK_V], U32, "z_codes%d" % c) for c in range(CHUNKS)]
         z_planes = [tile([P, CHUNK_V], U8, "z_plane%d" % c) for c in range(CHUNKS)]
         y_f32 = [tile([P, PACK, CHUNK_V], F32, "y_f32_%d" % c) for c in range(CHUNKS)]
-        y_bf = [tile([P, CHUNK_V, PACK], BF16, "y_bf%d" % c) for c in range(CHUNKS)]
-        y_codes = tile([P, V], U32, "y_codes")
+        y_bf = {c: tile([P, CHUNK_V, PACK], BF16, "y_bf%d" % c) for c in (0, 1, 3)}
+        y_codes = {}
         y_plane = tile([P, V], U8, "y_plane")
         out_rows = out_0.rearrange("(p t) v -> p t v", t=PACK)
         words_out = out_1[0].rearrange("p c r -> p (c r)").bitcast(I32)
@@ -93,7 +104,7 @@ def tile_picked_scorepool_relu_po_kernel(
         def scores(c):
             banks = []
             for b in range(CHUNK_J // BANK_J):
-                bank = score_psum.tile([P, PACK, BANK_J], F32, name="score_bank")
+                bank = psum.tile([P, PACK, BANK_J], F32, name="bank")
                 cols = slice(b * BANK_J, (b + 1) * BANK_J)
                 for t in range(PACK):
                     keys = slice(t * P, (t + 1) * P)
@@ -118,6 +129,8 @@ def tile_picked_scorepool_relu_po_kernel(
 
         def pool(c, b):
             rows = slice(b * BANK_V, (b + 1) * BANK_V)
+            if b == 0:
+                pooled[c] = tile([P, CHUNK_V, PACK], F32, "pooled%d" % c, "pooled%d" % (c % 2))
             nc.vector.scalar_tensor_tensor(
                 pooled[c][:, rows, :],
                 score_banks[c][b][:, :, 1:BANK_J:2].rearrange("p t v -> p v t"),
@@ -127,10 +140,16 @@ def tile_picked_scorepool_relu_po_kernel(
                 ALU.max,
             )
 
+        def weigh_head(c):
+            nc.gpsimd.tensor_tensor(z_bf[c][:, :POOL_V, :], pooled[c][:, :POOL_V, :], gains[:], ALU.mult)
+
         def weigh(c):
-            engine = nc.vector
-            engine.tensor_tensor(
-                z_bf[c][:], pooled[c][:], gains[:].unsqueeze(1).to_broadcast([P, CHUNK_V, PACK]), ALU.mult
+            first = POOL_V
+            nc.vector.tensor_tensor(
+                z_bf[c][:, first:, :],
+                pooled[c][:, first:, :],
+                gain_bank[:, 0, :].unsqueeze(1).to_broadcast([P, CHUNK_V - first, PACK]),
+                ALU.mult,
             )
 
         def product(c, bank, first, count):
@@ -145,39 +164,38 @@ def tile_picked_scorepool_relu_po_kernel(
                     stop=True,
                 )
 
-        def values(c):
+        def quantise_z(c):
             nc.vector.quantize_mx(
                 out=z_codes[c][:].bitcast(FP8X4), scales=z_planes[c][:], in_=z_bf[c][:].rearrange("p v t -> p (v t)")
             )
-            cols = slice(c * CHUNK_V, (c + 1) * CHUNK_V)
-            if c < CHUNKS - 1:
-                bank = out_psum.tile([P, PACK, CHUNK_V], F32, name="out_bank")
-                product(c, bank, 0, PACK)
-                nc.scalar.copy(y_f32[c][:], bank[:])
-                nc.sync.dma_start(out_rows[:, :, cols], y_f32[c][:])
-                nc.scalar.copy(y_bf[c][:], bank[:].rearrange("p t v -> p v t"))
-            else:
-                low = out_psum.tile([P, 2, CHUNK_V], F32, name="out_bank")
-                product(c, low, 0, 2)
-                nc.scalar.copy(y_f32[c][:, 0:2, :], low[:])
-                nc.sync.dma_start(out_rows[:, 0:2, cols], y_f32[c][:, 0:2, :])
-                nc.scalar.copy(y_bf[c][:, :, 0:2], low[:].rearrange("p t v -> p v t"))
-                high = out_psum.tile([P, 2, CHUNK_V], F32, name="out_bank")
-                product(c, high, 2, 2)
-                nc.vector.tensor_copy(y_bf[c][:, :, 2:4], high[:].rearrange("p t v -> p v t"))
-                nc.vector.tensor_copy(y_f32[c][:, 2:4, :], high[:])
-                nc.scalar.dma_start(out_rows[:, 2:4, cols], y_f32[c][:, 2:4, :])
+
+        def values(c, first=0, count=PACK):
+            bank = psum.tile([P, count, CHUNK_V], F32, name="bank")
+            product(c, bank, first, count)
+            return bank
+
+        def keep_f32(copy, c, bank, rows=slice(0, PACK)):
+            copy(y_f32[c][:, rows, :], bank[:])
+
+        def round_out(copy, c, bank, rows=slice(0, PACK)):
+            copy(y_bf[c][:, :, rows], bank[:].rearrange("p t v -> p v t"))
+
+        def store_f32(c, queue, rows=slice(0, PACK)):
+            queue.dma_start(out_rows[:, rows, c * CHUNK_V : (c + 1) * CHUNK_V], y_f32[c][:, rows, :])
 
         def quantise_out(c):
-            cols = slice(c * CHUNK_V, (c + 1) * CHUNK_V)
             nc.vector.quantize_mx(
-                out=y_codes[:, cols].bitcast(FP8X4), scales=y_plane[:, cols], in_=y_bf[c][:].rearrange("p v t -> p (v t)")
+                out=y_codes[c].bitcast(FP8X4),
+                scales=y_plane[:, c * CHUNK_V : (c + 1) * CHUNK_V],
+                in_=y_bf[c][:].rearrange("p v t -> p (v t)"),
             )
 
-        def store_words(first, stop):
-            cols = slice(first * CHUNK_V, stop * CHUNK_V)
-            nc.sync.dma_start(words_out[:, cols], y_codes[:, cols].bitcast(I32))
-
+        nc.scalar.copy(gains[:], gain_cols[:].unsqueeze(1).to_broadcast([P, POOL_V, PACK]))
+        turn_bank = psum.tile([P, P], F32, name="bank")
+        nc.tensor.transpose(turn_bank[:], gains[:, :TURN_V, :].rearrange("p v t -> p (v t)"), identity[:])
+        nc.scalar.copy(gains_turned[:], turn_bank[:])
+        gain_bank = gain_psum.tile([P, TURN_V, PACK], F32, name="gain_bank")
+        nc.tensor.transpose(gain_bank[:].rearrange("p v t -> p (v t)"), gains_turned[:], identity[:])
         key_halves = [slice(h * H // 2, (h + 1) * H // 2) for h in range(2)]
         key_lists = [kidx_sb[:, keys.start // LIST : keys.stop // LIST] for keys in key_halves]
         x_scales_picked = tile([P, S], U8, "x_scales_picked")
@@ -190,7 +208,6 @@ def tile_picked_scorepool_relu_po_kernel(
         to_plane(d_plane, nc.scalar)
         for r in range(4):
             nc.sync.dma_start(x_plane[r:P:32, :].bitcast(I32), x_scales_picked[8 * r : P : 32, :].bitcast(I32))
-        nc.sync.dma_start(gains[:], gn.rearrange("(p t) o -> p (t o)", t=PACK))
         nc.sync.dma_start(w_words_in[:].bitcast(I32), w1_words[0].bitcast(I32))
         for keys, entries in zip(key_halves, key_lists):
             nc.vector.tensor_copy(d_picked[:, keys], d_word_table[:].indirect(entries))
@@ -208,28 +225,56 @@ def tile_picked_scorepool_relu_po_kernel(
         for c in range(2):
             pick_words(c, c + 1)
             score_banks.append(scores(c))
-        w_codes = tile([P, 2 * N], U8, "w_codes", "x_codes1")
+        pick_words(2, 4)
+        score_banks.append(scores(2))
+        pool(0, 0)
+        weigh_head(0)
+        pool(0, 1)
+        w_codes = tile([P, 2 * N], U8, "w_codes", "first0_1")
         nc.scalar.copy(
             w_codes[:].bitcast(U16).rearrange("p (t m) -> p t m", t=PACK),
             w_words_in[:].bitcast(U16).rearrange("p (m t) -> p t m", t=PACK),
         )
-        pick_words(2, 4)
-        score_banks.extend(scores(c) for c in range(2, 4))
-        pool(0, 0)
-        pool(0, 1)
+        score_banks.append(scores(3))
+        low, high = slice(0, 2), slice(2, 4)
         for c in range(CHUNKS - 1):
             pool(c + 1, 0)
+            weigh_head(c + 1)
             weigh(c)
             pool(c + 1, 1)
-            values(c)
-        quantise_out(0)
+            quantise_z(c)
+            if c < CHUNKS - 2:
+                bank = values(c)
+                keep_f32(nc.scalar.copy, c, bank)
+                store_f32(c, nc.sync)
+                round_out(nc.scalar.copy, c, bank)
+        banks = values(2, 0, 2), values(2, 2, 2)
+        keep_f32(nc.scalar.copy, 2, banks[0], low)
+        keep_f32(nc.scalar.copy, 2, banks[1], high)
+        store_f32(2, nc.sync)
         weigh(3)
+        first_words = tile([P, CHUNK_V], U32, "first_words", "first3_1")
+        y_codes[0] = first_words[:]
+        quantise_out(0)
+        nc.sync.dma_start(words_out[:, :CHUNK_V], first_words[:].bitcast(I32))
+        quantise_z(3)
+        other_words = last.tile([P, V - CHUNK_V], U32, name="other_words", align_bytes=64, offset=1024)
+        for c in range(1, CHUNKS):
+            y_codes[c] = other_words[:, (c - 1) * CHUNK_V : c * CHUNK_V]
+        y_bf[2] = last.tile([P, CHUNK_V, PACK], BF16, name="y_bf2", align_bytes=64, offset=0)
         quantise_out(1)
-        store_words(0, 2)
-        values(3)
+        round_out(nc.vector.tensor_copy, 2, banks[0], low)
+        round_out(nc.scalar.copy, 2, banks[1], high)
+        banks = values(3, 0, 2), values(3, 2, 2)
+        keep_f32(nc.vector.tensor_copy, 3, banks[0], low)
+        store_f32(3, nc.sync, low)
+        keep_f32(nc.scalar.copy, 3, banks[1], high)
+        store_f32(3, nc.scalar, high)
+        round_out(nc.vector.tensor_copy, 3, banks[0], low)
+        round_out(nc.scalar.copy, 3, banks[1], high)
         quantise_out(2)
         quantise_out(3)
-        store_words(2, 4)
+        nc.sync.dma_start(words_out[:, CHUNK_V:], other_words[:].bitcast(I32))
         for q in range(4):
             queue = nc.scalar if q % 2 == 0 else nc.sync
             queue.dma_start(out_2[0, 4 * q : 4 * q + 4, :].bitcast(I32), y_plane[32 * q : 32 * q + 4, :].bitcast(I32))

@@ -24,9 +24,8 @@ SCORE_SCALE = 0.0625
 CHUNK_V = 128
 CHUNK_J = 2 * CHUNK_V
 CHUNKS = V // CHUNK_V
-BANK_J = 128
-BANK_V = BANK_J // 2
-POOL_V = 32
+PAIR = 2
+POOL_V = (48, 48, 48, 0)
 TURN_V = P // PACK
 
 
@@ -52,7 +51,7 @@ def tile_picked_scorepool_relu_po_kernel(
         d_word_table = tile([P, G], U32, "d_word_table")
         w_words_in = tile([P, 2 * N], U8, "w_words_in")
         gain_cols = tile([P, PACK], F32, "gain_cols")
-        gains = tile([P, POOL_V, PACK], F32, "gains")
+        gains = tile([P, max(POOL_V), PACK], F32, "gains")
         gains_turned = tile([P, P], F32, "gains_turned")
         identity = tile([P, P], F32, "identity")
 
@@ -103,24 +102,23 @@ def tile_picked_scorepool_relu_po_kernel(
 
         def scores(c):
             banks = []
-            for b in range(CHUNK_J // BANK_J):
-                bank = psum.tile([P, PACK, BANK_J], F32, name="bank")
-                cols = slice(b * BANK_J, (b + 1) * BANK_J)
-                for t in range(PACK):
-                    keys = slice(t * P, (t + 1) * P)
+            for b in range(PACK // PAIR):
+                bank = psum.tile([P, PAIR, CHUNK_J], F32, name="bank")
+                for i in range(PAIR):
+                    keys = slice((PAIR * b + i) * P, (PAIR * b + i + 1) * P)
                     nc.tensor.matmul_mx(
-                        out=bank[:, t, :],
+                        out=bank[:, i, :],
                         lhsT=d_codes[:, keys].bitcast(FP8X4),
                         lhsT_scale=d_plane[:, keys],
-                        rhs=x_codes[c][:, cols].bitcast(FP8X4),
-                        rhs_scale=x_plane[:, c * CHUNK_J + b * BANK_J : c * CHUNK_J + (b + 1) * BANK_J],
+                        rhs=x_codes[c].bitcast(FP8X4),
+                        rhs_scale=x_plane[:, c * CHUNK_J : (c + 1) * CHUNK_J],
                         start=True,
                         stop=True,
                     )
-                firsts[c, b] = tile([P, BANK_V, PACK], F32, "first%d_%d" % (c, b))
+                firsts[c, b] = tile([P, CHUNK_V, PAIR], F32, "first%d_%d" % (c, b))
                 nc.scalar.activation(
                     firsts[c, b][:],
-                    bank[:, :, 0:BANK_J:2].rearrange("p t v -> p v t"),
+                    bank[:, :, 0:CHUNK_J:2].rearrange("p t v -> p v t"),
                     ACT.Relu,
                     scale=SCORE_SCALE,
                 )
@@ -128,27 +126,35 @@ def tile_picked_scorepool_relu_po_kernel(
             return banks
 
         def pool(c, b):
-            rows = slice(b * BANK_V, (b + 1) * BANK_V)
             if b == 0:
-                pooled[c] = tile([P, CHUNK_V, PACK], F32, "pooled%d" % c, "pooled%d" % (c % 2))
+                pooled[c] = tile([P, PACK // PAIR, CHUNK_V, PAIR], F32, "pooled%d" % c, "pooled%d" % (c % 2))
             nc.vector.scalar_tensor_tensor(
-                pooled[c][:, rows, :],
-                score_banks[c][b][:, :, 1:BANK_J:2].rearrange("p t v -> p v t"),
+                pooled[c][:, b],
+                score_banks[c][b][:, :, 1:CHUNK_J:2].rearrange("p t v -> p v t"),
                 SCORE_SCALE,
                 firsts[c, b][:],
                 ALU.mult,
                 ALU.max,
             )
 
+        def by_pairs(ap):
+            return ap.rearrange("p v (b i) -> p v b i", i=PAIR)
+
         def weigh_head(c):
-            nc.gpsimd.tensor_tensor(z_bf[c][:, :POOL_V, :], pooled[c][:, :POOL_V, :], gains[:], ALU.mult)
+            head = slice(0, POOL_V[c])
+            nc.gpsimd.tensor_tensor(
+                by_pairs(z_bf[c][:, head, :]),
+                pooled[c][:, :, head, :].rearrange("p b v i -> p v b i"),
+                by_pairs(gains[:, head, :]),
+                ALU.mult,
+            )
 
         def weigh(c):
-            first = POOL_V
+            rest = slice(POOL_V[c], CHUNK_V)
             nc.vector.tensor_tensor(
-                z_bf[c][:, first:, :],
-                pooled[c][:, first:, :],
-                gain_bank[:, 0, :].unsqueeze(1).to_broadcast([P, CHUNK_V - first, PACK]),
+                by_pairs(z_bf[c][:, rest, :]),
+                pooled[c][:, :, rest, :].rearrange("p b v i -> p v b i"),
+                by_pairs(gain_bank[:, 0, :].unsqueeze(1).to_broadcast([P, CHUNK_V - POOL_V[c], PACK])),
                 ALU.mult,
             )
 
@@ -190,7 +196,7 @@ def tile_picked_scorepool_relu_po_kernel(
                 in_=y_bf[c][:].rearrange("p v t -> p (v t)"),
             )
 
-        nc.scalar.copy(gains[:], gain_cols[:].unsqueeze(1).to_broadcast([P, POOL_V, PACK]))
+        nc.scalar.copy(gains[:], gain_cols[:].unsqueeze(1).to_broadcast([P, max(POOL_V), PACK]))
         turn_bank = psum.tile([P, P], F32, name="bank")
         nc.tensor.transpose(turn_bank[:], gains[:, :TURN_V, :].rearrange("p v t -> p (v t)"), identity[:])
         nc.scalar.copy(gains_turned[:], turn_bank[:])
@@ -228,8 +234,8 @@ def tile_picked_scorepool_relu_po_kernel(
         pick_words(2, 4)
         score_banks.append(scores(2))
         pool(0, 0)
-        weigh_head(0)
         pool(0, 1)
+        weigh_head(0)
         w_codes = tile([P, 2 * N], U8, "w_codes", "first0_1")
         nc.scalar.copy(
             w_codes[:].bitcast(U16).rearrange("p (t m) -> p t m", t=PACK),
@@ -239,10 +245,11 @@ def tile_picked_scorepool_relu_po_kernel(
         low, high = slice(0, 2), slice(2, 4)
         for c in range(CHUNKS - 1):
             pool(c + 1, 0)
-            weigh_head(c + 1)
             weigh(c)
             pool(c + 1, 1)
             quantise_z(c)
+            if POOL_V[c + 1]:
+                weigh_head(c + 1)
             if c < CHUNKS - 2:
                 bank = values(c)
                 keep_f32(nc.scalar.copy, c, bank)

@@ -25,6 +25,7 @@ CHUNK_V = 128
 CHUNK_J = 2 * CHUNK_V
 CHUNKS = V // CHUNK_V
 PAIR = 2
+LINE = 4
 POOL_V = (48, 48, 48, 0)
 TURN_V = P // PACK
 
@@ -223,8 +224,8 @@ def tile_picked_scorepool_relu_po_kernel(
         )
         for keys in key_halves:
             nc.vector.tensor_copy(
-                d_codes[:].rearrange("p (t m) -> p m t", t=PACK)[:, keys.start // PACK : keys.stop // PACK, :],
-                d_picked[:, keys].rearrange("p (m t) -> p m t", t=PACK),
+                d_codes[:].rearrange("p (t c i) -> p c t i", t=PACK, i=LINE)[:, keys.start // 16 : keys.stop // 16],
+                d_picked[:, keys].rearrange("p (c i t) -> p c t i", t=PACK, i=LINE),
             )
         to_plane(w_plane, nc.sync)
         score_banks = []

@@ -26,7 +26,7 @@ CHUNK_J = 2 * CHUNK_V
 CHUNKS = V // CHUNK_V
 PAIR = 2
 LINE = 4
-POOL_V = (48, 48, 48, 0)
+POOL_V = (60, 60, 60, 0)
 TURN_V = P // PACK
 
 

@@ -26,7 +26,7 @@ CHUNK_J = 2 * CHUNK_V
 CHUNKS = V // CHUNK_V
 PAIR = 2
 LINE = 4
-POOL_V = (60, 60, 60, 0)
+POOL_V = (44, 68, 68, 0)
 TURN_V = P // PACK
 
 

@@ -26,7 +26,7 @@ CHUNK_J = 2 * CHUNK_V
 CHUNKS = V // CHUNK_V
 PAIR = 2
 LINE = 4
-POOL_V = (44, 68, 68, 0)
+POOL_V = (60, 60, 60, 0)
 TURN_V = P // PACK
 
 
@@ -67,9 +67,9 @@ def tile_picked_scorepool_relu_po_kernel(
         nc.sync.dma_start(kidx_sb[:], kidx)
         nc.sync.dma_start(d_scale_table[0:P:8, :].bitcast(I32), d_scales[0].bitcast(I32))
         nc.sync.dma_start(offs_sb[:], offs)
+        nc.sync.dma_start(gain_cols[:], gn.rearrange("(p t) o -> p (t o)", t=PACK))
         nc.sync.dma_start(w_scale_rows[0:P:8, :].bitcast(I32), w1_scales[0].bitcast(I32))
         nc.scalar.dma_start(x_scale_table[0:P:8, :].bitcast(I32), x_scales[0].bitcast(I32))
-        nc.scalar.dma_start(gain_cols[:], gn.rearrange("(p t) o -> p (t o)", t=PACK))
         nc.sync.dma_start(d_word_table[:].bitcast(I32), d_words[0].rearrange("p c r -> p (c r)").bitcast(I32))
         nc.sync.dma_start(x_word_table[:].bitcast(I32), x_words[0].rearrange("p c r -> p (c r)").bitcast(I32))
 
@@ -277,7 +277,7 @@ def tile_picked_scorepool_relu_po_kernel(
         keep_f32(nc.vector.tensor_copy, 3, banks[0], low)
         store_f32(3, nc.sync, low)
         keep_f32(nc.scalar.copy, 3, banks[1], high)
-        store_f32(3, nc.scalar, high)
+        store_f32(3, nc.sync, high)
         round_out(nc.vector.tensor_copy, 3, banks[0], low)
         round_out(nc.scalar.copy, 3, banks[1], high)
         quantise_out(2)

@@ -261,28 +261,26 @@ def tile_picked_scorepool_relu_po_kernel(
         keep_f32(nc.scalar.copy, 2, banks[1], high)
         store_f32(2, nc.sync)
         weigh(3)
-        first_words = tile([P, CHUNK_V], U32, "first_words", "first3_1")
-        y_codes[0] = first_words[:]
+        first_words = tile([P, V // 2], U32, "first_words", "first3_1")
+        y_codes[0], y_codes[1] = first_words[:, :CHUNK_V], first_words[:, CHUNK_V:]
         quantise_out(0)
-        nc.sync.dma_start(words_out[:, :CHUNK_V], first_words[:].bitcast(I32))
         quantise_z(3)
-        other_words = last.tile([P, V - CHUNK_V], U32, name="other_words", align_bytes=64, offset=1024)
-        for c in range(1, CHUNKS):
-            y_codes[c] = other_words[:, (c - 1) * CHUNK_V : c * CHUNK_V]
+        other_words = last.tile([P, V // 2], U32, name="other_words", align_bytes=64, offset=1024)
+        y_codes[2], y_codes[3] = other_words[:, :CHUNK_V], other_words[:, CHUNK_V:]
         y_bf[2] = last.tile([P, CHUNK_V, PACK], BF16, name="y_bf2", align_bytes=64, offset=0)
         quantise_out(1)
+        nc.sync.dma_start(words_out[:, : V // 2], first_words[:].bitcast(I32))
         round_out(nc.vector.tensor_copy, 2, banks[0], low)
         round_out(nc.scalar.copy, 2, banks[1], high)
         banks = values(3, 0, 2), values(3, 2, 2)
         keep_f32(nc.vector.tensor_copy, 3, banks[0], low)
-        store_f32(3, nc.sync, low)
         keep_f32(nc.scalar.copy, 3, banks[1], high)
-        store_f32(3, nc.sync, high)
+        store_f32(3, nc.sync)
         round_out(nc.vector.tensor_copy, 3, banks[0], low)
         round_out(nc.scalar.copy, 3, banks[1], high)
         quantise_out(2)
         quantise_out(3)
-        nc.sync.dma_start(words_out[:, CHUNK_V:], other_words[:].bitcast(I32))
+        nc.sync.dma_start(words_out[:, V // 2 :], other_words[:].bitcast(I32))
         for q in range(4):
             queue = nc.scalar if q % 2 == 0 else nc.sync
             queue.dma_start(out_2[0, 4 * q : 4 * q + 4, :].bitcast(I32), y_plane[32 * q : 32 * q + 4, :].bitcast(I32))

@@ -20,14 +20,19 @@ ACT = mybir.ActivationFunctionType
 P = 128
 PACK = 4
 LIST = 16
+QUAD = 32
+LIVE = 4
+ROW_STEP = 8
 SCORE_SCALE = 0.0625
 CHUNK_V = 128
 CHUNK_J = 2 * CHUNK_V
 CHUNKS = V // CHUNK_V
 PAIR = 2
 LINE = 4
-POOL_V = (60, 60, 60, 0)
+RING = 7
+POOL_V = (60, 60, 52, 0)
 TURN_V = P // PACK
+Y_BF2_AT, Z_BF3_AT, OTHER_WORDS_AT = 0, 512, 1024
 
 
 def tile_picked_scorepool_relu_po_kernel(
@@ -38,7 +43,7 @@ def tile_picked_scorepool_relu_po_kernel(
         keep = ctx.enter_context(tc.tile_pool(name="keep", bufs=1))
         last = ctx.enter_context(tc.tile_pool(name="last", bufs=1))
         gain_psum = ctx.enter_context(tc.psum_pool(name="gain_psum", bufs=1))
-        psum = ctx.enter_context(tc.psum_pool(name="psum", bufs=7))
+        psum = ctx.enter_context(tc.psum_pool(name="psum", bufs=RING))
 
         def tile(shape, dtype, name, tag=""):
             return keep.tile(shape, dtype, name=name, tag=tag or name, align_bytes=64)
@@ -65,11 +70,11 @@ def tile_picked_scorepool_relu_po_kernel(
         make_identity(nc, identity[:], nomemset=True)
 
         nc.sync.dma_start(kidx_sb[:], kidx)
-        nc.sync.dma_start(d_scale_table[0:P:8, :].bitcast(I32), d_scales[0].bitcast(I32))
+        nc.sync.dma_start(d_scale_table[0:P:ROW_STEP, :].bitcast(I32), d_scales[0].bitcast(I32))
         nc.sync.dma_start(offs_sb[:], offs)
         nc.sync.dma_start(gain_cols[:], gn.rearrange("(p t) o -> p (t o)", t=PACK))
-        nc.sync.dma_start(w_scale_rows[0:P:8, :].bitcast(I32), w1_scales[0].bitcast(I32))
-        nc.scalar.dma_start(x_scale_table[0:P:8, :].bitcast(I32), x_scales[0].bitcast(I32))
+        nc.sync.dma_start(w_scale_rows[0:P:ROW_STEP, :].bitcast(I32), w1_scales[0].bitcast(I32))
+        nc.scalar.dma_start(x_scale_table[0:P:ROW_STEP, :].bitcast(I32), x_scales[0].bitcast(I32))
         nc.sync.dma_start(d_word_table[:].bitcast(I32), d_words[0].rearrange("p c r -> p (c r)").bitcast(I32))
         nc.sync.dma_start(x_word_table[:].bitcast(I32), x_words[0].rearrange("p c r -> p (c r)").bitcast(I32))
 
@@ -77,10 +82,9 @@ def tile_picked_scorepool_relu_po_kernel(
         d_plane = tile([P, H], U8, "d_plane")
         d_picked = tile([P, H], U32, "d_picked")
         d_codes = tile([P, H], U32, "d_codes")
-        x_codes, x_planes, firsts = {}, {}, {}
-        pooled = {}
+        x_codes, firsts, pooled = {}, {}, {}
         z_bf = [tile([P, CHUNK_V, PACK], BF16, "z_bf%d" % c) for c in range(CHUNKS - 1)]
-        z_bf.append(last.tile([P, CHUNK_V, PACK], BF16, name="z_bf3", align_bytes=64, offset=512))
+        z_bf.append(last.tile([P, CHUNK_V, PACK], BF16, name="z_bf3", align_bytes=64, offset=Z_BF3_AT))
         z_codes = [tile([P, CHUNK_V], U32, "z_codes%d" % c) for c in range(CHUNKS)]
         z_planes = [tile([P, CHUNK_V], U8, "z_plane%d" % c) for c in range(CHUNKS)]
         y_f32 = [tile([P, PACK, CHUNK_V], F32, "y_f32_%d" % c) for c in range(CHUNKS)]
@@ -91,8 +95,8 @@ def tile_picked_scorepool_relu_po_kernel(
         words_out = out_1[0].rearrange("p c r -> p (c r)").bitcast(I32)
 
         def to_plane(plane, queue):
-            for r in range(1, 4):
-                queue.dma_start(plane[r:P:32, :].bitcast(I32), plane[8 * r : P : 32, :].bitcast(I32))
+            for r in range(1, LIVE):
+                queue.dma_start(plane[r:P:QUAD, :].bitcast(I32), plane[ROW_STEP * r : P : QUAD, :].bitcast(I32))
 
         def pick_words(first, stop):
             picked = tile([P, (stop - first) * CHUNK_J], U32, "x_codes%d" % first)
@@ -159,7 +163,13 @@ def tile_picked_scorepool_relu_po_kernel(
                 ALU.mult,
             )
 
-        def product(c, bank, first, count):
+        def quantise_z(c):
+            nc.vector.quantize_mx(
+                out=z_codes[c][:].bitcast(FP8X4), scales=z_planes[c][:], in_=z_bf[c][:].rearrange("p v t -> p (v t)")
+            )
+
+        def values(c, first=0, count=PACK):
+            bank = psum.tile([P, count, CHUNK_V], F32, name="bank")
             for t in range(first, first + count):
                 nc.tensor.matmul_mx(
                     out=bank[:, t - first, :],
@@ -170,15 +180,6 @@ def tile_picked_scorepool_relu_po_kernel(
                     start=True,
                     stop=True,
                 )
-
-        def quantise_z(c):
-            nc.vector.quantize_mx(
-                out=z_codes[c][:].bitcast(FP8X4), scales=z_planes[c][:], in_=z_bf[c][:].rearrange("p v t -> p (v t)")
-            )
-
-        def values(c, first=0, count=PACK):
-            bank = psum.tile([P, count, CHUNK_V], F32, name="bank")
-            product(c, bank, first, count)
             return bank
 
         def keep_f32(copy, c, bank, rows=slice(0, PACK)):
@@ -187,8 +188,8 @@ def tile_picked_scorepool_relu_po_kernel(
         def round_out(copy, c, bank, rows=slice(0, PACK)):
             copy(y_bf[c][:, :, rows], bank[:].rearrange("p t v -> p v t"))
 
-        def store_f32(c, queue, rows=slice(0, PACK)):
-            queue.dma_start(out_rows[:, rows, c * CHUNK_V : (c + 1) * CHUNK_V], y_f32[c][:, rows, :])
+        def store_f32(c):
+            nc.sync.dma_start(out_rows[:, :, c * CHUNK_V : (c + 1) * CHUNK_V], y_f32[c][:])
 
         def quantise_out(c):
             nc.vector.quantize_mx(
@@ -203,6 +204,7 @@ def tile_picked_scorepool_relu_po_kernel(
         nc.scalar.copy(gains_turned[:], turn_bank[:])
         gain_bank = gain_psum.tile([P, TURN_V, PACK], F32, name="gain_bank")
         nc.tensor.transpose(gain_bank[:].rearrange("p v t -> p (v t)"), gains_turned[:], identity[:])
+
         key_halves = [slice(h * H // 2, (h + 1) * H // 2) for h in range(2)]
         key_lists = [kidx_sb[:, keys.start // LIST : keys.stop // LIST] for keys in key_halves]
         x_scales_picked = tile([P, S], U8, "x_scales_picked")
@@ -213,9 +215,12 @@ def tile_picked_scorepool_relu_po_kernel(
         )
         nc.vector.tensor_copy(x_scales_picked[:, S // 2 :], x_scale_table[:].indirect(offs_sb[:, S // 2 // LIST :]))
         to_plane(d_plane, nc.scalar)
-        for r in range(4):
-            nc.sync.dma_start(x_plane[r:P:32, :].bitcast(I32), x_scales_picked[8 * r : P : 32, :].bitcast(I32))
+        for r in range(LIVE):
+            nc.sync.dma_start(
+                x_plane[r:P:QUAD, :].bitcast(I32), x_scales_picked[ROW_STEP * r : P : QUAD, :].bitcast(I32)
+            )
         nc.sync.dma_start(w_words_in[:].bitcast(I32), w1_words[0].bitcast(I32))
+
         for keys, entries in zip(key_halves, key_lists):
             nc.vector.tensor_copy(d_picked[:, keys], d_word_table[:].indirect(entries))
         w_plane = tile([P, N], U8, "w_plane")
@@ -223,16 +228,18 @@ def tile_picked_scorepool_relu_po_kernel(
             w_plane[:].rearrange("p (t m) -> p t m", t=PACK), w_scale_rows[:].rearrange("p (m t) -> p t m", t=PACK)
         )
         for keys in key_halves:
+            lines = slice(keys.start // (LINE * PACK), keys.stop // (LINE * PACK))
             nc.vector.tensor_copy(
-                d_codes[:].rearrange("p (t c i) -> p c t i", t=PACK, i=LINE)[:, keys.start // 16 : keys.stop // 16],
+                d_codes[:].rearrange("p (t c i) -> p c t i", t=PACK, i=LINE)[:, lines],
                 d_picked[:, keys].rearrange("p (c i t) -> p c t i", t=PACK, i=LINE),
             )
         to_plane(w_plane, nc.sync)
+
         score_banks = []
         for c in range(2):
             pick_words(c, c + 1)
             score_banks.append(scores(c))
-        pick_words(2, 4)
+        pick_words(2, CHUNKS)
         score_banks.append(scores(2))
         pool(0, 0)
         pool(0, 1)
@@ -243,7 +250,8 @@ def tile_picked_scorepool_relu_po_kernel(
             w_words_in[:].bitcast(U16).rearrange("p (m t) -> p t m", t=PACK),
         )
         score_banks.append(scores(3))
-        low, high = slice(0, 2), slice(2, 4)
+
+        low, high = slice(0, PAIR), slice(PAIR, PACK)
         for c in range(CHUNKS - 1):
             pool(c + 1, 0)
             weigh(c)
@@ -254,33 +262,36 @@ def tile_picked_scorepool_relu_po_kernel(
             if c < CHUNKS - 2:
                 bank = values(c)
                 keep_f32(nc.scalar.copy, c, bank)
-                store_f32(c, nc.sync)
+                store_f32(c)
                 round_out(nc.scalar.copy, c, bank)
-        banks = values(2, 0, 2), values(2, 2, 2)
+
+        banks = values(2, low.start, PAIR), values(2, high.start, PAIR)
         keep_f32(nc.scalar.copy, 2, banks[0], low)
         keep_f32(nc.scalar.copy, 2, banks[1], high)
-        store_f32(2, nc.sync)
+        store_f32(2)
         weigh(3)
         first_words = tile([P, V // 2], U32, "first_words", "first3_1")
         y_codes[0], y_codes[1] = first_words[:, :CHUNK_V], first_words[:, CHUNK_V:]
         quantise_out(0)
         quantise_z(3)
-        other_words = last.tile([P, V // 2], U32, name="other_words", align_bytes=64, offset=1024)
+        other_words = last.tile([P, V // 2], U32, name="other_words", align_bytes=64, offset=OTHER_WORDS_AT)
         y_codes[2], y_codes[3] = other_words[:, :CHUNK_V], other_words[:, CHUNK_V:]
-        y_bf[2] = last.tile([P, CHUNK_V, PACK], BF16, name="y_bf2", align_bytes=64, offset=0)
+        y_bf[2] = last.tile([P, CHUNK_V, PACK], BF16, name="y_bf2", align_bytes=64, offset=Y_BF2_AT)
         quantise_out(1)
         nc.sync.dma_start(words_out[:, : V // 2], first_words[:].bitcast(I32))
         round_out(nc.vector.tensor_copy, 2, banks[0], low)
         round_out(nc.scalar.copy, 2, banks[1], high)
-        banks = values(3, 0, 2), values(3, 2, 2)
+        banks = values(3, low.start, PAIR), values(3, high.start, PAIR)
         keep_f32(nc.vector.tensor_copy, 3, banks[0], low)
         keep_f32(nc.scalar.copy, 3, banks[1], high)
-        store_f32(3, nc.sync)
+        store_f32(3)
         round_out(nc.vector.tensor_copy, 3, banks[0], low)
         round_out(nc.scalar.copy, 3, banks[1], high)
         quantise_out(2)
         quantise_out(3)
         nc.sync.dma_start(words_out[:, V // 2 :], other_words[:].bitcast(I32))
-        for q in range(4):
+        for q in range(P // QUAD):
             queue = nc.scalar if q % 2 == 0 else nc.sync
-            queue.dma_start(out_2[0, 4 * q : 4 * q + 4, :].bitcast(I32), y_plane[32 * q : 32 * q + 4, :].bitcast(I32))
+            queue.dma_start(
+                out_2[0, LIVE * q : LIVE * (q + 1), :].bitcast(I32), y_plane[QUAD * q : QUAD * q + LIVE, :].bitcast(I32)
+            )

from contextlib import ExitStack

import concourse.mybir as mybir
from concourse.masks import make_identity

K, T, S, V, N, G, H = 512, 2048, 1024, 512, 512, 2048, 512
FLOPS = 2 * K * H * S + 2 * H * N * V

F32 = mybir.dt.float32
BF16 = mybir.dt.bfloat16
I32 = mybir.dt.int32
U32 = mybir.dt.uint32
U16 = mybir.dt.uint16
U8 = mybir.dt.uint8
FP8X4 = mybir.dt.float8_e4m3fn_x4
FP4X4 = mybir.dt.float4_e2m1fn_x4
ALU = mybir.AluOpType
ACT = mybir.ActivationFunctionType

P = 128
PACK = 4
LIST = 16
QUAD = 32
LIVE = 4
ROW_STEP = 8
SCORE_SCALE = 0.0625
CHUNK_V = 128
CHUNK_J = 2 * CHUNK_V
CHUNKS = V // CHUNK_V
PAIR = 2
LINE = 4
RING = 7
POOL_V = (60, 60, 52, 0)
TURN_V = P // PACK
Y_BF2_AT, Z_BF3_AT, OTHER_WORDS_AT = 0, 512, 1024


def tile_picked_scorepool_relu_po_kernel(
    tc, x_words, x_scales, d_words, d_scales, gn, w1_words, w1_scales, offs, kidx, out_0, out_1, out_2
):
    nc = tc.nc
    with ExitStack() as ctx:
        keep = ctx.enter_context(tc.tile_pool(name="keep", bufs=1))
        last = ctx.enter_context(tc.tile_pool(name="last", bufs=1))
        gain_psum = ctx.enter_context(tc.psum_pool(name="gain_psum", bufs=1))
        psum = ctx.enter_context(tc.psum_pool(name="psum", bufs=RING))

        def tile(shape, dtype, name, tag=""):
            return keep.tile(shape, dtype, name=name, tag=tag or name, align_bytes=64)

        kidx_sb = keep.tile([P, H // LIST], U16, name="kidx_sb")
        offs_sb = keep.tile([P, S // LIST], U16, name="offs_sb")
        d_scale_table = tile([P, G], U8, "d_scale_table")
        x_word_table = tile([P, T], U32, "x_word_table")
        x_scale_table = tile([P, T], U8, "x_scale_table")
        w_scale_rows = tile([P, N], U8, "w_scale_rows")
        d_word_table = tile([P, G], U32, "d_word_table")
        w_words_in = tile([P, 2 * N], U8, "w_words_in")
        gain_cols = tile([P, PACK], F32, "gain_cols")
        gains = tile([P, max(POOL_V), PACK], F32, "gains")
        gains_turned = tile([P, P], F32, "gains_turned")
        identity = tile([P, P], F32, "identity")

        x_plane = tile([P, S], U8, "x_plane")
        nc.vector.memset(d_scale_table[:].bitcast(I32), 0)
        nc.vector.memset(x_scale_table[:].bitcast(I32), 0)
        nc.vector.memset(w_scale_rows[:].bitcast(I32), 0)
        nc.vector.memset(x_plane[:].bitcast(I32), 0)
        nc.vector.memset(identity[:], 0.0)
        make_identity(nc, identity[:], nomemset=True)

        nc.sync.dma_start(kidx_sb[:], kidx)
        nc.sync.dma_start(d_scale_table[0:P:ROW_STEP, :].bitcast(I32), d_scales[0].bitcast(I32))
        nc.sync.dma_start(offs_sb[:], offs)
        nc.sync.dma_start(gain_cols[:], gn.rearrange("(p t) o -> p (t o)", t=PACK))
        nc.sync.dma_start(w_scale_rows[0:P:ROW_STEP, :].bitcast(I32), w1_scales[0].bitcast(I32))
        nc.scalar.dma_start(x_scale_table[0:P:ROW_STEP, :].bitcast(I32), x_scales[0].bitcast(I32))
        nc.sync.dma_start(d_word_table[:].bitcast(I32), d_words[0].rearrange("p c r -> p (c r)").bitcast(I32))
        nc.sync.dma_start(x_word_table[:].bitcast(I32), x_words[0].rearrange("p c r -> p (c r)").bitcast(I32))

        d_scales_picked = tile([P, H], U8, "d_scales_picked")
        d_plane = tile([P, H], U8, "d_plane")
        d_picked = tile([P, H], U32, "d_picked")
        d_codes = tile([P, H], U32, "d_codes")
        x_codes, firsts, pooled = {}, {}, {}
        z_bf = [tile([P, CHUNK_V, PACK], BF16, "z_bf%d" % c) for c in range(CHUNKS - 1)]
        z_bf.append(last.tile([P, CHUNK_V, PACK], BF16, name="z_bf3", align_bytes=64, offset=Z_BF3_AT))
        z_codes = [tile([P, CHUNK_V], U32, "z_codes%d" % c) for c in range(CHUNKS)]
        z_planes = [tile([P, CHUNK_V], U8, "z_plane%d" % c) for c in range(CHUNKS)]
        y_f32 = [tile([P, PACK, CHUNK_V], F32, "y_f32_%d" % c) for c in range(CHUNKS)]
        y_bf = {c: tile([P, CHUNK_V, PACK], BF16, "y_bf%d" % c) for c in (0, 1, 3)}
        y_codes = {}
        y_plane = tile([P, V], U8, "y_plane")
        out_rows = out_0.rearrange("(p t) v -> p t v", t=PACK)
        words_out = out_1[0].rearrange("p c r -> p (c r)").bitcast(I32)

        def to_plane(plane, queue):
            for r in range(1, LIVE):
                queue.dma_start(plane[r:P:QUAD, :].bitcast(I32), plane[ROW_STEP * r : P : QUAD, :].bitcast(I32))

        def pick_words(first, stop):
            picked = tile([P, (stop - first) * CHUNK_J], U32, "x_codes%d" % first)
            entries = offs_sb[:, first * CHUNK_J // LIST : stop * CHUNK_J // LIST]
            nc.vector.tensor_copy(picked[:], x_word_table[:].indirect(entries))
            for c in range(first, stop):
                x_codes[c] = picked[:, (c - first) * CHUNK_J : (c - first + 1) * CHUNK_J]

        def scores(c):
            banks = []
            for b in range(PACK // PAIR):
                bank = psum.tile([P, PAIR, CHUNK_J], F32, name="bank")
                for i in range(PAIR):
                    keys = slice((PAIR * b + i) * P, (PAIR * b + i + 1) * P)
                    nc.tensor.matmul_mx(
                        out=bank[:, i, :],
                        lhsT=d_codes[:, keys].bitcast(FP8X4),
                        lhsT_scale=d_plane[:, keys],
                        rhs=x_codes[c].bitcast(FP8X4),
                        rhs_scale=x_plane[:, c * CHUNK_J : (c + 1) * CHUNK_J],
                        start=True,
                        stop=True,
                    )
                firsts[c, b] = tile([P, CHUNK_V, PAIR], F32, "first%d_%d" % (c, b))
                nc.scalar.activation(
                    firsts[c, b][:],
                    bank[:, :, 0:CHUNK_J:2].rearrange("p t v -> p v t"),
                    ACT.Relu,
                    scale=SCORE_SCALE,
                )
                banks.append(bank)
            return banks

        def pool(c, b):
            if b == 0:
                pooled[c] = tile([P, PACK // PAIR, CHUNK_V, PAIR], F32, "pooled%d" % c, "pooled%d" % (c % 2))
            nc.vector.scalar_tensor_tensor(
                pooled[c][:, b],
                score_banks[c][b][:, :, 1:CHUNK_J:2].rearrange("p t v -> p v t"),
                SCORE_SCALE,
                firsts[c, b][:],
                ALU.mult,
                ALU.max,
            )

        def by_pairs(ap):
            return ap.rearrange("p v (b i) -> p v b i", i=PAIR)

        def weigh_head(c):
            head = slice(0, POOL_V[c])
            nc.gpsimd.tensor_tensor(
                by_pairs(z_bf[c][:, head, :]),
                pooled[c][:, :, head, :].rearrange("p b v i -> p v b i"),
                by_pairs(gains[:, head, :]),
                ALU.mult,
            )

        def weigh(c):
            rest = slice(POOL_V[c], CHUNK_V)
            nc.vector.tensor_tensor(
                by_pairs(z_bf[c][:, rest, :]),
                pooled[c][:, :, rest, :].rearrange("p b v i -> p v b i"),
                by_pairs(gain_bank[:, 0, :].unsqueeze(1).to_broadcast([P, CHUNK_V - POOL_V[c], PACK])),
                ALU.mult,
            )

        def quantise_z(c):
            nc.vector.quantize_mx(
                out=z_codes[c][:].bitcast(FP8X4), scales=z_planes[c][:], in_=z_bf[c][:].rearrange("p v t -> p (v t)")
            )

        def values(c, first=0, count=PACK):
            bank = psum.tile([P, count, CHUNK_V], F32, name="bank")
            for t in range(first, first + count):
                nc.tensor.matmul_mx(
                    out=bank[:, t - first, :],
                    lhsT=w_codes[:, 2 * t * P : 2 * (t + 1) * P].bitcast(FP4X4),
                    lhsT_scale=w_plane[:, t * P : (t + 1) * P],
                    rhs=z_codes[c][:].bitcast(FP8X4),
                    rhs_scale=z_planes[c][:],
                    start=True,
                    stop=True,
                )
            return bank

        def keep_f32(copy, c, bank, rows=slice(0, PACK)):
            copy(y_f32[c][:, rows, :], bank[:])

        def round_out(copy, c, bank, rows=slice(0, PACK)):
            copy(y_bf[c][:, :, rows], bank[:].rearrange("p t v -> p v t"))

        def store_f32(c):
            nc.sync.dma_start(out_rows[:, :, c * CHUNK_V : (c + 1) * CHUNK_V], y_f32[c][:])

        def quantise_out(c):
            nc.vector.quantize_mx(
                out=y_codes[c].bitcast(FP8X4),
                scales=y_plane[:, c * CHUNK_V : (c + 1) * CHUNK_V],
                in_=y_bf[c][:].rearrange("p v t -> p (v t)"),
            )

        nc.scalar.copy(gains[:], gain_cols[:].unsqueeze(1).to_broadcast([P, max(POOL_V), PACK]))
        turn_bank = psum.tile([P, P], F32, name="bank")
        nc.tensor.transpose(turn_bank[:], gains[:, :TURN_V, :].rearrange("p v t -> p (v t)"), identity[:])
        nc.scalar.copy(gains_turned[:], turn_bank[:])
        gain_bank = gain_psum.tile([P, TURN_V, PACK], F32, name="gain_bank")
        nc.tensor.transpose(gain_bank[:].rearrange("p v t -> p (v t)"), gains_turned[:], identity[:])

        key_halves = [slice(h * H // 2, (h + 1) * H // 2) for h in range(2)]
        key_lists = [kidx_sb[:, keys.start // LIST : keys.stop // LIST] for keys in key_halves]
        x_scales_picked = tile([P, S], U8, "x_scales_picked")
        nc.vector.tensor_copy(d_scales_picked[:], d_scale_table[:].indirect(kidx_sb[:]))
        nc.vector.tensor_copy(x_scales_picked[:, : S // 2], x_scale_table[:].indirect(offs_sb[:, : S // 2 // LIST]))
        nc.vector.tensor_copy(
            d_plane[:].rearrange("p (t m) -> p t m", t=PACK), d_scales_picked[:].rearrange("p (m t) -> p t m", t=PACK)
        )
        nc.vector.tensor_copy(x_scales_picked[:, S // 2 :], x_scale_table[:].indirect(offs_sb[:, S // 2 // LIST :]))
        to_plane(d_plane, nc.scalar)
        for r in range(LIVE):
            nc.sync.dma_start(
                x_plane[r:P:QUAD, :].bitcast(I32), x_scales_picked[ROW_STEP * r : P : QUAD, :].bitcast(I32)
            )
        nc.sync.dma_start(w_words_in[:].bitcast(I32), w1_words[0].bitcast(I32))

        for keys, entries in zip(key_halves, key_lists):
            nc.vector.tensor_copy(d_picked[:, keys], d_word_table[:].indirect(entries))
        w_plane = tile([P, N], U8, "w_plane")
        nc.gpsimd.tensor_copy(
            w_plane[:].rearrange("p (t m) -> p t m", t=PACK), w_scale_rows[:].rearrange("p (m t) -> p t m", t=PACK)
        )
        for keys in key_halves:
            lines = slice(keys.start // (LINE * PACK), keys.stop // (LINE * PACK))
            nc.vector.tensor_copy(
                d_codes[:].rearrange("p (t c i) -> p c t i", t=PACK, i=LINE)[:, lines],
                d_picked[:, keys].rearrange("p (c i t) -> p c t i", t=PACK, i=LINE),
            )
        to_plane(w_plane, nc.sync)

        score_banks = []
        for c in range(2):
            pick_words(c, c + 1)
            score_banks.append(scores(c))
        pick_words(2, CHUNKS)
        score_banks.append(scores(2))
        pool(0, 0)
        pool(0, 1)
        weigh_head(0)
        w_codes = tile([P, 2 * N], U8, "w_codes", "first0_1")
        nc.scalar.copy(
            w_codes[:].bitcast(U16).rearrange("p (t m) -> p t m", t=PACK),
            w_words_in[:].bitcast(U16).rearrange("p (m t) -> p t m", t=PACK),
        )
        score_banks.append(scores(3))

        low, high = slice(0, PAIR), slice(PAIR, PACK)
        for c in range(CHUNKS - 1):
            pool(c + 1, 0)
            weigh(c)
            pool(c + 1, 1)
            quantise_z(c)
            if POOL_V[c + 1]:
                weigh_head(c + 1)
            if c < CHUNKS - 2:
                bank = values(c)
                keep_f32(nc.scalar.copy, c, bank)
                store_f32(c)
                round_out(nc.scalar.copy, c, bank)

        banks = values(2, low.start, PAIR), values(2, high.start, PAIR)
        keep_f32(nc.scalar.copy, 2, banks[0], low)
        keep_f32(nc.scalar.copy, 2, banks[1], high)
        store_f32(2)
        weigh(3)
        first_words = tile([P, V // 2], U32, "first_words", "first3_1")
        y_codes[0], y_codes[1] = first_words[:, :CHUNK_V], first_words[:, CHUNK_V:]
        quantise_out(0)
        quantise_z(3)
        other_words = last.tile([P, V // 2], U32, name="other_words", align_bytes=64, offset=OTHER_WORDS_AT)
        y_codes[2], y_codes[3] = other_words[:, :CHUNK_V], other_words[:, CHUNK_V:]
        y_bf[2] = last.tile([P, CHUNK_V, PACK], BF16, name="y_bf2", align_bytes=64, offset=Y_BF2_AT)
        quantise_out(1)
        nc.sync.dma_start(words_out[:, : V // 2], first_words[:].bitcast(I32))
        round_out(nc.vector.tensor_copy, 2, banks[0], low)
        round_out(nc.scalar.copy, 2, banks[1], high)
        banks = values(3, low.start, PAIR), values(3, high.start, PAIR)
        keep_f32(nc.vector.tensor_copy, 3, banks[0], low)
        keep_f32(nc.scalar.copy, 3, banks[1], high)
        store_f32(3)
        round_out(nc.vector.tensor_copy, 3, banks[0], low)
        round_out(nc.scalar.copy, 3, banks[1], high)
        quantise_out(2)
        quantise_out(3)
        nc.sync.dma_start(words_out[:, V // 2 :], other_words[:].bitcast(I32))
        for q in range(P // QUAD):
            queue = nc.scalar if q % 2 == 0 else nc.sync
            queue.dma_start(
                out_2[0, LIVE * q : LIVE * (q + 1), :].bitcast(I32), y_plane[QUAD * q : QUAD * q + LIVE, :].bitcast(I32)
            )
